import numpy as np
import ml_dtypes


def mxq(x, axis, fmt="e4m3"):
    dtype, down = {"e4m3": (ml_dtypes.float8_e4m3fn, 7), "e5m2": (ml_dtypes.float8_e5m2, 14)}[fmt]
    v = np.moveaxis(np.asarray(x, np.float32).astype(ml_dtypes.bfloat16).astype(np.float64), axis, -1)
    blocks = v.reshape(v.shape[:-1] + (-1, 32))
    amax = np.abs(blocks).max(-1, keepdims=True)
    byte = np.maximum(np.where(amax > 0, np.frexp(amax)[1] - 1 + 127, 0) - down, 1)
    scale = np.exp2(byte - 127.0)
    codes = (blocks / scale).astype(np.float32).astype(dtype).astype(np.float64)
    return np.moveaxis((codes * scale).reshape(v.shape), -1, axis)


WIDE = False


def mx_kscale(k):
    if not WIDE:
        return np.ones(k)
    levels = np.array([10, -10, 5, -5, 0])
    if k % 512:
        return np.exp2(np.random.permutation(np.resize(levels, k // 32))).repeat(32)
    a = np.empty((k // 512, 16))
    for p in range(k // 512):
        a[p, :8] = np.random.permutation(np.resize(levels, 8))
        for g in range(8):
            far = levels[np.abs(levels - a[p, g]) >= 10]
            a[p, g + 8] = far[np.random.randint(len(far))]
    return np.exp2(a.ravel()).repeat(32)


def f64(x):
    return np.asarray(x).astype(np.float64)


def striped8(idx):
    return np.concatenate([x.reshape(-1, 16).T for x in idx]).astype(np.uint16)


def runs(offs, k):
    lists = np.stack([offs[16 * r : 16 * r + 16].T.reshape(-1) for r in range(8)]).astype(np.int64)
    return lists[np.arange(k) % 512 // 64]


def pack_weight(w):
    k, n = w.shape
    w = f64(np.asarray(w, np.float32).astype(ml_dtypes.bfloat16)).reshape(k // 32, 32, n)
    amax = np.abs(w).max(1)
    byte = np.clip(np.where(amax > 0, np.frexp(amax)[1] - 1 + 127 - 7, 1), 1, 254)
    scaled = (w * np.exp2(127.0 - byte)[:, None, :]).reshape(k, n).astype(np.float32)
    words = np.ascontiguousarray(scaled.reshape(k // 512, 128, 4, n).transpose(0, 1, 3, 2)).astype(ml_dtypes.float8_e4m3fn).view(np.uint8)
    return words, np.ascontiguousarray(byte.astype(np.uint8).reshape(k // 512, 16, n))


def unpack_weight(words, scales):
    g, p, n, _ = words.shape
    vals = np.ascontiguousarray(words).view(ml_dtypes.float8_e4m3fn).astype(np.float64) * np.repeat(np.exp2(scales.astype(np.float64) - 127.0), 8, axis=1)[..., None]
    return vals.transpose(0, 1, 3, 2).reshape(g * 512, n)

def planes(y):
    n, m = y.shape
    v = y.astype(np.float32).astype(ml_dtypes.bfloat16).astype(np.float64).reshape(n // 32, 32, m)
    top = np.abs(v).max(1)
    byte = np.clip(np.where(top > 0, np.frexp(top)[1] - 1 + 127 - 7, 1), 1, 254)
    codes = (v * np.exp2(127.0 - byte)[:, None, :]).reshape(n, m).astype(np.float32).astype(ml_dtypes.float8_e4m3fn).view(np.uint8)
    words = codes.reshape(n // 512, 128, 4, m).transpose(0, 1, 3, 2)
    return np.ascontiguousarray(words), np.ascontiguousarray(byte.astype(np.uint8).reshape(n // 512, 16, m))


K, T, S, N, U = 512, 2048, 512, 512, 1024


def setup_inputs():
    n = np.random.standard_normal
    s = mx_kscale(K)[:, None]
    packed_xT = pack_weight(n((K, T)) * s)
    return {
        "x_words": packed_xT[0],
        "x_scales": packed_xT[1],
        "w1": (n((K, N)) / np.sqrt(K) / s).astype(np.float32),
        "par": n((N, U)).astype(np.float32),
        "ssq": np.random.uniform(0.5, 3.0, (N, U)).astype(np.float32),
        "offs": striped8(np.stack([np.random.permutation(T)[:S] for _ in range(8)])),
        "ent": striped8(np.stack([np.random.permutation(U)[:S] for _ in range(8)])),
    }


def reference(x_words, x_scales, w1, par, ssq, offs, ent):
    xq = unpack_weight(x_words, x_scales)[np.arange(K)[:, None], runs(offs, K)]
    y = mxq(f64(w1), 0, "e4m3").T @ xq
    b = np.sqrt(f64(ssq)[np.arange(N)[:, None], runs(ent, N)] + (y) ** 2)
    pn = f64(par)[np.arange(N)[:, None], runs(ent, N)] - (y / b)
    out = f64(par).copy()
    out[np.arange(N)[:, None], runs(ent, N)] = pn
    return (out,) + planes(out)

@@ -1,0 +1,179 @@
+from contextlib import ExitStack
+
+import concourse.mybir as mybir
+
+K, T, S, N, U = 512, 2048, 512, 512, 1024
+FLOPS = 2 * K * N * S
+
+F32 = mybir.dt.float32
+BF16 = mybir.dt.bfloat16
+I32 = mybir.dt.int32
+U32 = mybir.dt.uint32
+U16 = mybir.dt.uint16
+U8 = mybir.dt.uint8
+FP8X4 = mybir.dt.float8_e4m3fn_x4
+ALU = mybir.AluOpType
+ACT = mybir.ActivationFunctionType
+
+P = 128
+PACK = 4
+W_CHUNKS = 2
+OUT_CHUNKS = 4
+ORDER = (2, 0, 1, 3)
+SLOT = 4096
+PAR_SLOT = (2, 5, 3, 4)
+SSQ_SLOT = (3, 4, 0, 1)
+
+
+def tile_picked_adagr8_none_po_kernel(
+    tc, x_words, x_scales, w1, par, ssq, offs, ent, out_0, out_1, out_2
+):
+    nc = tc.nc
+    with ExitStack() as ctx:
+        lists = ctx.enter_context(tc.tile_pool(name="lists", bufs=1))
+        held = ctx.enter_context(tc.tile_pool(name="held", bufs=1))
+        ring = ctx.enter_context(tc.tile_pool(name="ring", bufs=2))
+        arena = ctx.enter_context(tc.tile_pool(name="arena", bufs=1))
+        psum = ctx.enter_context(tc.psum_pool(name="psum", bufs=1))
+
+        offs_sb = lists.tile([P, S // 16], U16, name="offs_sb")
+        ent_sb = lists.tile([P, S // 16], U16, name="ent_sb")
+
+        wc = N // W_CHUNKS
+        w_rows = w1.rearrange("(p j) c -> p j c", j=PACK)
+        w_raw = [
+            arena.tile([P, PACK, wc], F32, name="w_raw%d" % h, offset=(2 + h) * SLOT) for h in range(W_CHUNKS)
+        ]
+        nc.sync.dma_start(w_raw[0][:], w_rows[:, :, :wc])
+        nc.sync.dma_start(offs_sb[:], offs)
+
+        scale_win = arena.tile([P, T], U8, name="scale_win", align_bytes=64, offset=5 * SLOT)
+        nc.vector.memset(scale_win[:].bitcast(I32), 0)
+        for e in range(2):
+            nc.sync.dma_start(scale_win[e:P:16, :].bitcast(I32), x_scales[0, e:16:2, :].bitcast(I32))
+        warm = held.tile([P, 1], F32, name="warm")
+        warm_out = held.tile([P, 1], F32, name="warm_out")
+        nc.gpsimd.memset(warm[:], 1.0)
+        nc.scalar.activation(warm_out[:], warm[:], ACT.Abs_reciprocal_sqrt)
+
+        nc.sync.dma_start(w_raw[1][:], w_rows[:, :, wc:])
+        word_win = arena.tile([P, T], I32, name="word_win", align_bytes=64, offset=0)
+        nc.sync.dma_start(word_win[:], x_words[0].rearrange("p n t -> p (n t)").bitcast(I32))
+        nc.sync.dma_start(ent_sb[:], ent)
+
+        par_rows = par.rearrange("(p t) u -> p t u", t=PACK)
+        ssq_rows = ssq.rearrange("(p t) u -> p t u", t=PACK)
+        out_rows = out_0.rearrange("(p t) u -> p t u", t=PACK)
+
+        scale_got = held.tile([P, S], U8, name="scale_got", align_bytes=64)
+        nc.vector.tensor_copy(scale_got[:], scale_win[:].indirect(offs_sb[:]))
+        x_scale = held.tile([P, S], U8, name="x_scale", align_bytes=64)
+        nc.vector.tensor_copy(x_scale[:].bitcast(I32), scale_got[:].bitcast(I32))
+        for e in range(2):
+            nc.sync.dma_start(x_scale[2 + e : P : 32, :].bitcast(I32), scale_got[16 + e : P : 32, :].bitcast(I32))
+
+        w_bf = arena.tile([P, PACK, P, PACK], BF16, name="w_bf", align_bytes=64, offset=4 * SLOT)
+        mc = wc // PACK
+        for h in range(W_CHUNKS):
+            dst = w_bf[:, :, h * mc : (h + 1) * mc, :].rearrange("p t m j -> p m t j")
+            src = w_raw[h][:].rearrange("p j (m t) -> p m t j", t=PACK)
+            if h == 0:
+                nc.scalar.copy(dst, src)
+            else:
+                nc.vector.tensor_copy(dst, src)
+        w_codes = held.tile([P, N], U32, name="w_codes", align_bytes=64)
+        w_scale = held.tile([P, N], U8, name="w_scale", align_bytes=64)
+
+        out_bf = held.tile([P, U, PACK], BF16, name="out_bf", align_bytes=64)
+
+        y = {}
+        y2 = {}
+        nc.vector.quantize_mx(
+            out=w_codes[:].bitcast(FP8X4),
+            scales=w_scale[:],
+            in_=w_bf[:].rearrange("p t m j -> p (t m j)"),
+        )
+
+        x_codes = arena.tile([P, S], U32, name="x_codes", align_bytes=64, offset=5 * SLOT)
+        nc.vector.tensor_copy(x_codes[:], word_win[:].bitcast(U32).indirect(offs_sb[:]))
+
+        for t in ORDER:
+            cols = slice(t * P, (t + 1) * P)
+            y[t] = psum.tile([P, S], F32, name="y%d" % t)
+            nc.tensor.matmul_mx(
+                out=y[t][:],
+                lhsT=w_codes[:, cols].bitcast(FP8X4),
+                lhsT_scale=w_scale[:, cols],
+                rhs=x_codes[:].bitcast(FP8X4),
+                rhs_scale=x_scale[:],
+                start=True,
+                stop=True,
+            )
+            y2[t] = held.tile([P, S], F32, name="y2_%d" % t)
+            nc.scalar.activation(y2[t][:], y[t][:], ACT.Square)
+
+        par_win = {}
+        par_got = {}
+        rs = {}
+
+        def par_stage(t):
+            par_win[t] = arena.tile([P, U], F32, name="par_win%d" % t, offset=PAR_SLOT[ORDER.index(t)] * SLOT)
+            nc.sync.dma_start(par_win[t][:], par_rows[:, t, :])
+            par_got[t] = ring.tile([P, S], F32, name="par_got")
+            nc.vector.tensor_copy(par_got[t][:], par_win[t][:].indirect(ent_sb[:]))
+
+        def ssq_stage(t):
+            ssq_win = arena.tile([P, U], F32, name="ssq_win%d" % t, offset=SSQ_SLOT[ORDER.index(t)] * SLOT)
+            nc.sync.dma_start(ssq_win[:], ssq_rows[:, t, :])
+            tot = ring.tile([P, S], F32, name="tot")
+            nc.vector.tensor_tensor(tot[:], ssq_win[:].indirect(ent_sb[:]), y2[t][:], ALU.add)
+            rs[t] = held.tile([P, S], F32, name="rs%d" % t)
+            nc.scalar.activation(rs[t][:], tot[:], ACT.Abs_reciprocal_sqrt)
+
+        step = {}
+
+        def step_stage(t):
+            step[t] = ring.tile([P, S], F32, name="step")
+            nc.vector.scalar_tensor_tensor(step[t][:], y[t][:], -1.0, rs[t][:], ALU.mult, ALU.mult)
+
+        def put_stage(t):
+            nc.vector.tensor_tensor(par_win[t][:].indirect(ent_sb[:]), par_got[t][:], step[t][:], ALU.add)
+            nc.sync.dma_start(out_rows[:, t, :], par_win[t][:])
+
+        par_stage(ORDER[0])
+        ssq_stage(ORDER[0])
+        ssq_stage(ORDER[1])
+        step_stage(ORDER[0])
+        ssq_stage(ORDER[2])
+        put_stage(ORDER[0])
+        ssq_stage(ORDER[3])
+        for i in range(1, PACK):
+            nc.scalar.copy(out_bf[:, :, ORDER[i - 1]], par_win[ORDER[i - 1]][:])
+            step_stage(ORDER[i])
+            par_stage(ORDER[i])
+            put_stage(ORDER[i])
+
+        last = ORDER[-1]
+        oc = U // OUT_CHUNKS
+        chunks = [slice(c * oc, (c + 1) * oc) for c in range(OUT_CHUNKS)]
+        for cols in chunks[OUT_CHUNKS // 2 :]:
+            nc.scalar.copy(out_bf[:, cols, last], par_win[last][:, cols])
+        for cols in chunks[: OUT_CHUNKS // 2]:
+            nc.vector.tensor_copy(out_bf[:, cols, last], par_win[last][:, cols])
+
+        out_codes = held.tile([P, U], U32, name="out_codes", align_bytes=64)
+        out_scale = held.tile([P, U], U8, name="out_scale", align_bytes=64)
+        words_hbm = out_1[0].rearrange("p n t -> p (n t)").bitcast(I32)
+        stored = 0
+        for c, cols in enumerate(chunks):
+            nc.vector.quantize_mx(
+                out=out_codes[:, cols].bitcast(FP8X4),
+                scales=out_scale[:, cols],
+                in_=out_bf[:, cols, :].rearrange("p u t -> p (u t)"),
+            )
+            if c > 0:
+                nc.sync.dma_start(words_hbm[:, stored : cols.stop], out_codes[:, stored : cols.stop].bitcast(I32))
+                stored = cols.stop
+        for q in range(4):
+            eng = nc.scalar if q % 2 == 0 else nc.sync
+            eng.dma_start(out_2[0, 4 * q : 4 * q + 4, :].bitcast(I32), out_scale[32 * q : 32 * q + 4, :].bitcast(I32))

@@ -21,8 +21,8 @@ W_CHUNKS = 2
 OUT_CHUNKS = 4
 ORDER = (2, 0, 1, 3)
 SLOT = 4096
-PAR_SLOT = (2, 5, 3, 4)
-SSQ_SLOT = (3, 4, 0, 1)
+PAR_SLOT = (2, 3, 4, 0)
+SSQ_SLOT = (4, 0, 1, 5)
 
 
 def tile_picked_adagr8_none_po_kernel(
@@ -115,43 +115,66 @@ def tile_picked_adagr8_none_po_kernel(
         par_win = {}
         par_got = {}
         rs = {}
+        y_sb = {}
+        new = {}
 
         def par_stage(t):
             par_win[t] = arena.tile([P, U], F32, name="par_win%d" % t, offset=PAR_SLOT[ORDER.index(t)] * SLOT)
             nc.sync.dma_start(par_win[t][:], par_rows[:, t, :])
-            par_got[t] = ring.tile([P, S], F32, name="par_got")
+            par_got[t] = held.tile([P, S], F32, name="par_got%d" % t)
             nc.vector.tensor_copy(par_got[t][:], par_win[t][:].indirect(ent_sb[:]))
 
         def ssq_stage(t):
             ssq_win = arena.tile([P, U], F32, name="ssq_win%d" % t, offset=SSQ_SLOT[ORDER.index(t)] * SLOT)
             nc.sync.dma_start(ssq_win[:], ssq_rows[:, t, :])
-            tot = ring.tile([P, S], F32, name="tot")
-            nc.vector.tensor_tensor(tot[:], ssq_win[:].indirect(ent_sb[:]), y2[t][:], ALU.add)
+            if t != ORDER[-1]:
+                tot = ring.tile([P, S], F32, name="tot")
+                nc.vector.tensor_tensor(tot[:], ssq_win[:].indirect(ent_sb[:]), y2[t][:], ALU.add)
+                root(t, tot)
+            else:
+                ssq_last = held.tile([P, S], F32, name="ssq_last")
+                nc.vector.tensor_copy(ssq_last[:], ssq_win[:].indirect(ent_sb[:]))
+                return ssq_last
+
+        def root(t, tot):
             rs[t] = held.tile([P, S], F32, name="rs%d" % t)
             nc.scalar.activation(rs[t][:], tot[:], ACT.Abs_reciprocal_sqrt)
 
-        step = {}
+        def copy_y(t, tag):
+            y_sb[t] = held.tile([P, S], F32, name="y_sb%d" % t, tag=tag)
+            nc.scalar.copy(y_sb[t][:], y[t][:])
 
-        def step_stage(t):
-            step[t] = ring.tile([P, S], F32, name="step")
-            nc.vector.scalar_tensor_tensor(step[t][:], y[t][:], -1.0, rs[t][:], ALU.mult, ALU.mult)
+        def update(t):
+            step = arena.tile([P, S], F32, name="step%d" % t, offset=SSQ_SLOT[-2] * SLOT)
+            nc.gpsimd.tensor_tensor(step[:], y_sb[t][:], rs[t][:], ALU.mult)
+            if t == ORDER[-1]:
+                new[t] = arena.tile([P, S], F32, name="new%d" % t, offset=PAR_SLOT[0] * SLOT)
+            else:
+                new[t] = held.tile([P, S], F32, name="new%d" % t)
+            nc.gpsimd.tensor_tensor(new[t][:], par_got[t][:], step[:], ALU.subtract)
 
         def put_stage(t):
-            nc.vector.tensor_tensor(par_win[t][:].indirect(ent_sb[:]), par_got[t][:], step[t][:], ALU.add)
+            nc.vector.tensor_copy(par_win[t][:].indirect(ent_sb[:]), new[t][:])
             nc.sync.dma_start(out_rows[:, t, :], par_win[t][:])
 
         par_stage(ORDER[0])
-        ssq_stage(ORDER[0])
-        ssq_stage(ORDER[1])
-        step_stage(ORDER[0])
-        ssq_stage(ORDER[2])
-        put_stage(ORDER[0])
-        ssq_stage(ORDER[3])
-        for i in range(1, PACK):
-            nc.scalar.copy(out_bf[:, :, ORDER[i - 1]], par_win[ORDER[i - 1]][:])
-            step_stage(ORDER[i])
-            par_stage(ORDER[i])
-            put_stage(ORDER[i])
+        par_stage(ORDER[1])
+        for t in ORDER[:-1]:
+            ssq_stage(t)
+        ssq_last = ssq_stage(ORDER[-1])
+        for t in ORDER:
+            copy_y(t, "y_sb%d" % t)
+        for t in ORDER[2:]:
+            par_stage(t)
+        for i, t in enumerate(ORDER):
+            update(t)
+            if i == 0:
+                tot_last = arena.tile([P, S], F32, name="tot_last", offset=SSQ_SLOT[-2] * SLOT + SLOT // 2)
+                nc.gpsimd.tensor_tensor(tot_last[:], ssq_last[:], y2[ORDER[-1]][:], ALU.add)
+                root(ORDER[-1], tot_last)
+            put_stage(t)
+            if i + 1 < PACK:
+                nc.scalar.copy(out_bf[:, :, t], par_win[t][:])
 
         last = ORDER[-1]
         oc = U // OUT_CHUNKS

@@ -20,9 +20,9 @@ PACK = 4
 W_CHUNKS = 2
 OUT_CHUNKS = 4
 ORDER = (2, 0, 1, 3)
-SLOT = 4096
-PAR_SLOT = (2, 3, 4, 0)
-SSQ_SLOT = (4, 0, 1, 5)
+SLOT = 2048
+PAR_SLOT = (14, 18, 4, 0)
+SSQ_SLOT = (6, 8, 10, 12)
 
 
 def tile_picked_adagr8_none_po_kernel(
@@ -32,7 +32,6 @@ def tile_picked_adagr8_none_po_kernel(
     with ExitStack() as ctx:
         lists = ctx.enter_context(tc.tile_pool(name="lists", bufs=1))
         held = ctx.enter_context(tc.tile_pool(name="held", bufs=1))
-        ring = ctx.enter_context(tc.tile_pool(name="ring", bufs=2))
         arena = ctx.enter_context(tc.tile_pool(name="arena", bufs=1))
         psum = ctx.enter_context(tc.psum_pool(name="psum", bufs=1))
 
@@ -42,12 +41,12 @@ def tile_picked_adagr8_none_po_kernel(
         wc = N // W_CHUNKS
         w_rows = w1.rearrange("(p j) c -> p j c", j=PACK)
         w_raw = [
-            arena.tile([P, PACK, wc], F32, name="w_raw%d" % h, offset=(2 + h) * SLOT) for h in range(W_CHUNKS)
+            arena.tile([P, PACK, wc], F32, name="w_raw%d" % h, offset=(5 + 4 * h) * SLOT) for h in range(W_CHUNKS)
         ]
         nc.sync.dma_start(w_raw[0][:], w_rows[:, :, :wc])
         nc.sync.dma_start(offs_sb[:], offs)
 
-        scale_win = arena.tile([P, T], U8, name="scale_win", align_bytes=64, offset=5 * SLOT)
+        scale_win = arena.tile([P, T], U8, name="scale_win", align_bytes=64, offset=16 * SLOT)
         nc.vector.memset(scale_win[:].bitcast(I32), 0)
         for e in range(2):
             nc.sync.dma_start(scale_win[e:P:16, :].bitcast(I32), x_scales[0, e:16:2, :].bitcast(I32))
@@ -72,7 +71,7 @@ def tile_picked_adagr8_none_po_kernel(
         for e in range(2):
             nc.sync.dma_start(x_scale[2 + e : P : 32, :].bitcast(I32), scale_got[16 + e : P : 32, :].bitcast(I32))
 
-        w_bf = arena.tile([P, PACK, P, PACK], BF16, name="w_bf", align_bytes=64, offset=4 * SLOT)
+        w_bf = arena.tile([P, PACK, P, PACK], BF16, name="w_bf", align_bytes=64, offset=13 * SLOT)
         mc = wc // PACK
         for h in range(W_CHUNKS):
             dst = w_bf[:, :, h * mc : (h + 1) * mc, :].rearrange("p t m j -> p m t j")
@@ -84,7 +83,6 @@ def tile_picked_adagr8_none_po_kernel(
         w_codes = held.tile([P, N], U32, name="w_codes", align_bytes=64)
         w_scale = held.tile([P, N], U8, name="w_scale", align_bytes=64)
 
-        out_bf = held.tile([P, U, PACK], BF16, name="out_bf", align_bytes=64)
 
         y = {}
         y2 = {}
@@ -94,7 +92,7 @@ def tile_picked_adagr8_none_po_kernel(
             in_=w_bf[:].rearrange("p t m j -> p (t m j)"),
         )
 
-        x_codes = arena.tile([P, S], U32, name="x_codes", align_bytes=64, offset=5 * SLOT)
+        x_codes = arena.tile([P, S], U32, name="x_codes", align_bytes=64, offset=16 * SLOT)
         nc.vector.tensor_copy(x_codes[:], word_win[:].bitcast(U32).indirect(offs_sb[:]))
 
         for t in ORDER:
@@ -128,7 +126,7 @@ def tile_picked_adagr8_none_po_kernel(
             ssq_win = arena.tile([P, U], F32, name="ssq_win%d" % t, offset=SSQ_SLOT[ORDER.index(t)] * SLOT)
             nc.sync.dma_start(ssq_win[:], ssq_rows[:, t, :])
             if t != ORDER[-1]:
-                tot = ring.tile([P, S], F32, name="tot")
+                tot = held.tile([P, S], F32, name="tot%d" % t)
                 nc.vector.tensor_tensor(tot[:], ssq_win[:].indirect(ent_sb[:]), y2[t][:], ALU.add)
                 root(t, tot)
             else:
@@ -145,7 +143,7 @@ def tile_picked_adagr8_none_po_kernel(
             nc.scalar.copy(y_sb[t][:], y[t][:])
 
         def update(t):
-            step = arena.tile([P, S], F32, name="step%d" % t, offset=SSQ_SLOT[-2] * SLOT)
+            step = arena.tile([P, S], F32, name="step%d" % t, offset=11 * SLOT)
             nc.gpsimd.tensor_tensor(step[:], y_sb[t][:], rs[t][:], ALU.mult)
             if t == ORDER[-1]:
                 new[t] = arena.tile([P, S], F32, name="new%d" % t, offset=PAR_SLOT[0] * SLOT)
@@ -157,21 +155,22 @@ def tile_picked_adagr8_none_po_kernel(
             nc.vector.tensor_copy(par_win[t][:].indirect(ent_sb[:]), new[t][:])
             nc.sync.dma_start(out_rows[:, t, :], par_win[t][:])
 
-        par_stage(ORDER[0])
         par_stage(ORDER[1])
+        par_stage(ORDER[2])
         for t in ORDER[:-1]:
             ssq_stage(t)
         ssq_last = ssq_stage(ORDER[-1])
         for t in ORDER:
             copy_y(t, "y_sb%d" % t)
-        for t in ORDER[2:]:
-            par_stage(t)
+        par_stage(ORDER[0])
+        par_stage(ORDER[3])
         for i, t in enumerate(ORDER):
             update(t)
             if i == 0:
-                tot_last = arena.tile([P, S], F32, name="tot_last", offset=SSQ_SLOT[-2] * SLOT + SLOT // 2)
+                tot_last = arena.tile([P, S], F32, name="tot_last", offset=10 * SLOT)
                 nc.gpsimd.tensor_tensor(tot_last[:], ssq_last[:], y2[ORDER[-1]][:], ALU.add)
                 root(ORDER[-1], tot_last)
+                out_bf = arena.tile([P, U, PACK], BF16, name="out_bf", align_bytes=64, offset=7 * SLOT)
             put_stage(t)
             if i + 1 < PACK:
                 nc.scalar.copy(out_bf[:, :, t], par_win[t][:])

@@ -20,9 +20,15 @@ PACK = 4
 W_CHUNKS = 2
 OUT_CHUNKS = 4
 ORDER = (2, 0, 1, 3)
-SLOT = 2048
-PAR_SLOT = (14, 18, 4, 0)
-SSQ_SLOT = (6, 8, 10, 12)
+KB = 1024
+W_RAW_AT = (48, 16)
+W_BF_AT = 24
+WORD_AT = 66
+SCALE_AT = 44
+PAR_AT = (64, 10, 22, 40)
+SSQ_AT = (14, 18, 26, 68)
+STEP_AT = (57, 56, 58, 56)
+GOT_AT = (53, 62, 60, 63)
 
 
 def tile_picked_adagr8_none_po_kernel(
@@ -41,12 +47,12 @@ def tile_picked_adagr8_none_po_kernel(
         wc = N // W_CHUNKS
         w_rows = w1.rearrange("(p j) c -> p j c", j=PACK)
         w_raw = [
-            arena.tile([P, PACK, wc], F32, name="w_raw%d" % h, offset=(5 + 4 * h) * SLOT) for h in range(W_CHUNKS)
+            arena.tile([P, PACK, wc], F32, name="w_raw%d" % h, offset=W_RAW_AT[h] * KB) for h in range(W_CHUNKS)
         ]
         nc.sync.dma_start(w_raw[0][:], w_rows[:, :, :wc])
         nc.sync.dma_start(offs_sb[:], offs)
 
-        scale_win = arena.tile([P, T], U8, name="scale_win", align_bytes=64, offset=16 * SLOT)
+        scale_win = arena.tile([P, T], U8, name="scale_win", align_bytes=64, offset=SCALE_AT * KB)
         nc.vector.memset(scale_win[:].bitcast(I32), 0)
         for e in range(2):
             nc.sync.dma_start(scale_win[e:P:16, :].bitcast(I32), x_scales[0, e:16:2, :].bitcast(I32))
@@ -56,7 +62,7 @@ def tile_picked_adagr8_none_po_kernel(
         nc.scalar.activation(warm_out[:], warm[:], ACT.Abs_reciprocal_sqrt)
 
         nc.sync.dma_start(w_raw[1][:], w_rows[:, :, wc:])
-        word_win = arena.tile([P, T], I32, name="word_win", align_bytes=64, offset=0)
+        word_win = arena.tile([P, T], I32, name="word_win", align_bytes=64, offset=WORD_AT * KB)
         nc.sync.dma_start(word_win[:], x_words[0].rearrange("p n t -> p (n t)").bitcast(I32))
         nc.sync.dma_start(ent_sb[:], ent)
 
@@ -69,9 +75,9 @@ def tile_picked_adagr8_none_po_kernel(
         x_scale = held.tile([P, S], U8, name="x_scale", align_bytes=64)
         nc.vector.tensor_copy(x_scale[:].bitcast(I32), scale_got[:].bitcast(I32))
         for e in range(2):
-            nc.sync.dma_start(x_scale[2 + e : P : 32, :].bitcast(I32), scale_got[16 + e : P : 32, :].bitcast(I32))
+            nc.scalar.dma_start(x_scale[2 + e : P : 32, :].bitcast(I32), scale_got[16 + e : P : 32, :].bitcast(I32))
 
-        w_bf = arena.tile([P, PACK, P, PACK], BF16, name="w_bf", align_bytes=64, offset=13 * SLOT)
+        w_bf = arena.tile([P, PACK, P, PACK], BF16, name="w_bf", align_bytes=64, offset=W_BF_AT * KB)
         mc = wc // PACK
         for h in range(W_CHUNKS):
             dst = w_bf[:, :, h * mc : (h + 1) * mc, :].rearrange("p t m j -> p m t j")
@@ -92,88 +98,97 @@ def tile_picked_adagr8_none_po_kernel(
             in_=w_bf[:].rearrange("p t m j -> p (t m j)"),
         )
 
-        x_codes = arena.tile([P, S], U32, name="x_codes", align_bytes=64, offset=16 * SLOT)
-        nc.vector.tensor_copy(x_codes[:], word_win[:].bitcast(U32).indirect(offs_sb[:]))
+        x_codes = arena.tile([P, S], U32, name="x_codes", align_bytes=64, offset=(SCALE_AT - 1) * KB)
+        halves = [slice(h * S // 2, (h + 1) * S // 2) for h in range(2)]
+        for h, cols in enumerate(halves):
+            nc.vector.tensor_copy(x_codes[:, cols], word_win[:].bitcast(U32).indirect(offs_sb[:, h * 16 : (h + 1) * 16]))
 
-        for t in ORDER:
-            cols = slice(t * P, (t + 1) * P)
-            y[t] = psum.tile([P, S], F32, name="y%d" % t)
-            nc.tensor.matmul_mx(
-                out=y[t][:],
-                lhsT=w_codes[:, cols].bitcast(FP8X4),
-                lhsT_scale=w_scale[:, cols],
-                rhs=x_codes[:].bitcast(FP8X4),
-                rhs_scale=x_scale[:],
-                start=True,
-                stop=True,
-            )
+        y_sb = {}
+        for i, t in enumerate(ORDER):
+            rows = slice(t * P, (t + 1) * P)
             y2[t] = held.tile([P, S], F32, name="y2_%d" % t)
-            nc.scalar.activation(y2[t][:], y[t][:], ACT.Square)
+            y[t] = []
+            for cols in halves if i == 0 else [slice(0, S)]:
+                bank = psum.tile([P, cols.stop - cols.start], F32, name="y%d_%d" % (t, cols.start))
+                nc.tensor.matmul_mx(
+                    out=bank[:],
+                    lhsT=w_codes[:, rows].bitcast(FP8X4),
+                    lhsT_scale=w_scale[:, rows],
+                    rhs=x_codes[:, cols].bitcast(FP8X4),
+                    rhs_scale=x_scale[:, cols],
+                    start=True,
+                    stop=True,
+                )
+                nc.scalar.activation(y2[t][:, cols], bank[:], ACT.Square)
+                y[t].append((cols, bank))
 
         par_win = {}
         par_got = {}
         rs = {}
-        y_sb = {}
-        new = {}
+        step = {}
 
-        def par_stage(t):
-            par_win[t] = arena.tile([P, U], F32, name="par_win%d" % t, offset=PAR_SLOT[ORDER.index(t)] * SLOT)
+        def load_par(i):
+            t = ORDER[i]
+            par_win[t] = arena.tile([P, U], F32, name="par_win%d" % t, offset=PAR_AT[i] * KB)
             nc.sync.dma_start(par_win[t][:], par_rows[:, t, :])
-            par_got[t] = held.tile([P, S], F32, name="par_got%d" % t)
-            nc.vector.tensor_copy(par_got[t][:], par_win[t][:].indirect(ent_sb[:]))
 
-        def ssq_stage(t):
-            ssq_win = arena.tile([P, U], F32, name="ssq_win%d" % t, offset=SSQ_SLOT[ORDER.index(t)] * SLOT)
-            nc.sync.dma_start(ssq_win[:], ssq_rows[:, t, :])
-            if t != ORDER[-1]:
-                tot = held.tile([P, S], F32, name="tot%d" % t)
-                nc.vector.tensor_tensor(tot[:], ssq_win[:].indirect(ent_sb[:]), y2[t][:], ALU.add)
-                root(t, tot)
+        def fetch_par(i):
+            t = ORDER[i]
+            par_got[t] = arena.tile([P, S], F32, name="par_got%d" % t, offset=GOT_AT[i] * KB)
+            if i == 0:
+                nc.vector.tensor_tensor(par_got[t][:], par_win[t][:].indirect(ent_sb[:]), step[t][:], ALU.subtract)
             else:
-                ssq_last = held.tile([P, S], F32, name="ssq_last")
-                nc.vector.tensor_copy(ssq_last[:], ssq_win[:].indirect(ent_sb[:]))
-                return ssq_last
+                nc.vector.tensor_copy(par_got[t][:], par_win[t][:].indirect(ent_sb[:]))
 
-        def root(t, tot):
+        def fetch_ssq(i):
+            t = ORDER[i]
+            ssq_win = arena.tile([P, U], F32, name="ssq_win%d" % t, offset=SSQ_AT[i] * KB)
+            nc.sync.dma_start(ssq_win[:], ssq_rows[:, t, :])
+            tot = held.tile([P, S], F32, name="tot%d" % t)
+            nc.vector.tensor_tensor(tot[:], ssq_win[:].indirect(ent_sb[:]), y2[t][:], ALU.add)
             rs[t] = held.tile([P, S], F32, name="rs%d" % t)
             nc.scalar.activation(rs[t][:], tot[:], ACT.Abs_reciprocal_sqrt)
 
-        def copy_y(t, tag):
-            y_sb[t] = held.tile([P, S], F32, name="y_sb%d" % t, tag=tag)
-            nc.scalar.copy(y_sb[t][:], y[t][:])
+        def product(i):
+            t = ORDER[i]
+            step[t] = arena.tile([P, S], F32, name="step%d" % t, offset=STEP_AT[i] * KB)
+            nc.gpsimd.tensor_tensor(step[t][:], y_sb[t][:], rs[t][:], ALU.mult)
 
-        def update(t):
-            step = arena.tile([P, S], F32, name="step%d" % t, offset=11 * SLOT)
-            nc.gpsimd.tensor_tensor(step[:], y_sb[t][:], rs[t][:], ALU.mult)
-            if t == ORDER[-1]:
-                new[t] = arena.tile([P, S], F32, name="new%d" % t, offset=PAR_SLOT[0] * SLOT)
-            else:
-                new[t] = held.tile([P, S], F32, name="new%d" % t)
-            nc.gpsimd.tensor_tensor(new[t][:], par_got[t][:], step[:], ALU.subtract)
-
-        def put_stage(t):
-            nc.vector.tensor_copy(par_win[t][:].indirect(ent_sb[:]), new[t][:])
-            nc.sync.dma_start(out_rows[:, t, :], par_win[t][:])
-
-        par_stage(ORDER[1])
-        par_stage(ORDER[2])
-        for t in ORDER[:-1]:
-            ssq_stage(t)
-        ssq_last = ssq_stage(ORDER[-1])
-        for t in ORDER:
-            copy_y(t, "y_sb%d" % t)
-        par_stage(ORDER[0])
-        par_stage(ORDER[3])
-        for i, t in enumerate(ORDER):
-            update(t)
+        def put(i):
+            t = ORDER[i]
             if i == 0:
-                tot_last = arena.tile([P, S], F32, name="tot_last", offset=10 * SLOT)
-                nc.gpsimd.tensor_tensor(tot_last[:], ssq_last[:], y2[ORDER[-1]][:], ALU.add)
-                root(ORDER[-1], tot_last)
-                out_bf = arena.tile([P, U, PACK], BF16, name="out_bf", align_bytes=64, offset=7 * SLOT)
-            put_stage(t)
+                nc.vector.tensor_copy(par_win[t][:].indirect(ent_sb[:]), par_got[t][:])
+            else:
+                nc.vector.tensor_tensor(par_win[t][:].indirect(ent_sb[:]), par_got[t][:], step[t][:], ALU.add)
+            nc.sync.dma_start(out_rows[:, t, :], par_win[t][:])
             if i + 1 < PACK:
                 nc.scalar.copy(out_bf[:, :, t], par_win[t][:])
+
+        load_par(1)
+        fetch_par(1)
+        fetch_ssq(0)
+        fetch_ssq(1)
+        for i, t in enumerate(ORDER):
+            y_sb[t] = held.tile([P, S], F32, name="y_sb%d" % t)
+            for cols, bank in y[t]:
+                nc.scalar.activation(y_sb[t][:, cols], bank[:], ACT.Copy, scale=1.0 if i == 0 else -1.0)
+        load_par(2)
+        fetch_par(2)
+        product(0)
+        fetch_ssq(2)
+        fetch_ssq(3)
+        load_par(0)
+        fetch_par(0)
+        load_par(3)
+        product(1)
+        product(2)
+        out_bf = held.tile([P, U, PACK], BF16, name="out_bf", align_bytes=64)
+        put(0)
+        put(1)
+        fetch_par(3)
+        product(3)
+        put(2)
+        put(3)
 
         last = ORDER[-1]
         oc = U // OUT_CHUNKS

@@ -25,10 +25,14 @@ W_RAW_AT = (48, 16)
 W_BF_AT = 24
 WORD_AT = 66
 SCALE_AT = 44
-PAR_AT = (64, 10, 22, 40)
-SSQ_AT = (14, 18, 26, 68)
-STEP_AT = (57, 56, 58, 56)
-GOT_AT = (53, 62, 60, 63)
+PAR_AT = (64, 68, 10, 40)
+SSQ_AT = (14, 18, 26, 22)
+SQUARE_AT = (74, 76, 14, 16)
+Y_AT = (78, 18, 20, 76)
+STEP_AT = (90, 89, 88, 90)
+TOT_LAST_AT = 91
+OUT_BF_AT = 92
+GOT_AT = (52, 62, 60, 63)
 
 
 def tile_picked_adagr8_none_po_kernel(
@@ -103,10 +107,8 @@ def tile_picked_adagr8_none_po_kernel(
         for h, cols in enumerate(halves):
             nc.vector.tensor_copy(x_codes[:, cols], word_win[:].bitcast(U32).indirect(offs_sb[:, h * 16 : (h + 1) * 16]))
 
-        y_sb = {}
         for i, t in enumerate(ORDER):
             rows = slice(t * P, (t + 1) * P)
-            y2[t] = held.tile([P, S], F32, name="y2_%d" % t)
             y[t] = []
             for cols in halves if i == 0 else [slice(0, S)]:
                 bank = psum.tile([P, cols.stop - cols.start], F32, name="y%d_%d" % (t, cols.start))
@@ -119,35 +121,54 @@ def tile_picked_adagr8_none_po_kernel(
                     start=True,
                     stop=True,
                 )
-                nc.scalar.activation(y2[t][:, cols], bank[:], ACT.Square)
                 y[t].append((cols, bank))
 
+        y_sb = {}
         par_win = {}
         par_got = {}
+        ssq_win = {}
         rs = {}
         step = {}
+
+        def square(i):
+            t = ORDER[i]
+            y2[t] = arena.tile([P, S], F32, name="y2_%d" % t, offset=SQUARE_AT[i] * KB)
+            for cols, bank in y[t]:
+                nc.scalar.activation(y2[t][:, cols], bank[:], ACT.Square)
+
+        def copy_y(i):
+            t = ORDER[i]
+            y_sb[t] = arena.tile([P, S], F32, name="y_sb%d" % t, offset=Y_AT[i] * KB)
+            for cols, bank in y[t]:
+                nc.scalar.activation(y_sb[t][:, cols], bank[:], ACT.Copy, scale=1.0 if i < 2 else -1.0)
 
         def load_par(i):
             t = ORDER[i]
             par_win[t] = arena.tile([P, U], F32, name="par_win%d" % t, offset=PAR_AT[i] * KB)
             nc.sync.dma_start(par_win[t][:], par_rows[:, t, :])
 
+        def load_ssq(i):
+            t = ORDER[i]
+            ssq_win[t] = arena.tile([P, U], F32, name="ssq_win%d" % t, offset=SSQ_AT[i] * KB)
+            nc.sync.dma_start(ssq_win[t][:], ssq_rows[:, t, :])
+
         def fetch_par(i):
             t = ORDER[i]
             par_got[t] = arena.tile([P, S], F32, name="par_got%d" % t, offset=GOT_AT[i] * KB)
-            if i == 0:
+            if i < 2:
                 nc.vector.tensor_tensor(par_got[t][:], par_win[t][:].indirect(ent_sb[:]), step[t][:], ALU.subtract)
             else:
                 nc.vector.tensor_copy(par_got[t][:], par_win[t][:].indirect(ent_sb[:]))
 
-        def fetch_ssq(i):
-            t = ORDER[i]
-            ssq_win = arena.tile([P, U], F32, name="ssq_win%d" % t, offset=SSQ_AT[i] * KB)
-            nc.sync.dma_start(ssq_win[:], ssq_rows[:, t, :])
-            tot = held.tile([P, S], F32, name="tot%d" % t)
-            nc.vector.tensor_tensor(tot[:], ssq_win[:].indirect(ent_sb[:]), y2[t][:], ALU.add)
+        def root(t, tot):
             rs[t] = held.tile([P, S], F32, name="rs%d" % t)
             nc.scalar.activation(rs[t][:], tot[:], ACT.Abs_reciprocal_sqrt)
+
+        def fetch_ssq(i):
+            t = ORDER[i]
+            tot = held.tile([P, S], F32, name="tot%d" % t)
+            nc.vector.tensor_tensor(tot[:], ssq_win[t][:].indirect(ent_sb[:]), y2[t][:], ALU.add)
+            root(t, tot)
 
         def product(i):
             t = ORDER[i]
@@ -156,7 +177,7 @@ def tile_picked_adagr8_none_po_kernel(
 
         def put(i):
             t = ORDER[i]
-            if i == 0:
+            if i < 2:
                 nc.vector.tensor_copy(par_win[t][:].indirect(ent_sb[:]), par_got[t][:])
             else:
                 nc.vector.tensor_tensor(par_win[t][:].indirect(ent_sb[:]), par_got[t][:], step[t][:], ALU.add)
@@ -164,33 +185,44 @@ def tile_picked_adagr8_none_po_kernel(
             if i + 1 < PACK:
                 nc.scalar.copy(out_bf[:, :, t], par_win[t][:])
 
-        load_par(1)
-        fetch_par(1)
-        fetch_ssq(0)
-        fetch_ssq(1)
-        for i, t in enumerate(ORDER):
-            y_sb[t] = held.tile([P, S], F32, name="y_sb%d" % t)
-            for cols, bank in y[t]:
-                nc.scalar.activation(y_sb[t][:, cols], bank[:], ACT.Copy, scale=1.0 if i == 0 else -1.0)
+        last = ORDER[-1]
         load_par(2)
         fetch_par(2)
+        square(0)
+        square(1)
+        copy_y(0)
+        load_ssq(0)
+        fetch_ssq(0)
+        load_ssq(1)
+        fetch_ssq(1)
+        square(2)
+        square(3)
+        load_ssq(3)
+        ssq_last = held.tile([P, S], F32, name="ssq_last")
+        nc.vector.tensor_copy(ssq_last[:], ssq_win[last][:].indirect(ent_sb[:]))
         product(0)
+        load_ssq(2)
         fetch_ssq(2)
-        fetch_ssq(3)
+        for i in range(1, PACK):
+            copy_y(i)
         load_par(0)
         fetch_par(0)
+        load_par(1)
         load_par(3)
         product(1)
-        product(2)
-        out_bf = held.tile([P, U, PACK], BF16, name="out_bf", align_bytes=64)
+        tot_last = arena.tile([P, S], F32, name="tot_last", offset=TOT_LAST_AT * KB)
+        nc.gpsimd.tensor_tensor(tot_last[:], ssq_last[:], y2[last][:], ALU.add)
+        root(last, tot_last)
+        out_bf = arena.tile([P, U, PACK], BF16, name="out_bf", align_bytes=64, offset=OUT_BF_AT * KB)
         put(0)
+        fetch_par(1)
         put(1)
-        fetch_par(3)
+        product(2)
         product(3)
+        fetch_par(3)
         put(2)
         put(3)
 
-        last = ORDER[-1]
         oc = U // OUT_CHUNKS
         chunks = [slice(c * oc, (c + 1) * oc) for c in range(OUT_CHUNKS)]
         for cols in chunks[OUT_CHUNKS // 2 :]:

@@ -23,16 +23,16 @@ ORDER = (2, 0, 1, 3)
 KB = 1024
 W_RAW_AT = (48, 16)
 W_BF_AT = 24
-WORD_AT = 66
+WORD_AT = 78
 SCALE_AT = 44
-PAR_AT = (64, 68, 10, 40)
-SSQ_AT = (14, 18, 26, 22)
-SQUARE_AT = (74, 76, 14, 16)
-Y_AT = (78, 18, 20, 76)
-STEP_AT = (90, 89, 88, 90)
+PAR_AT = (84, 40, 10, 14)
+SSQ_AT = (18, 22, 78, 26)
+SQUARE_AT = (64, 62, 18, 20)
+Y_AT = (60, 22, 24, 62)
+STEP_AT = (90, 89, 90, 87)
 TOT_LAST_AT = 91
 OUT_BF_AT = 92
-GOT_AT = (52, 62, 60, 63)
+GOT_AT = (52, 54, 56, 58)
 
 
 def tile_picked_adagr8_none_po_kernel(
@@ -103,14 +103,12 @@ def tile_picked_adagr8_none_po_kernel(
         )
 
         x_codes = arena.tile([P, S], U32, name="x_codes", align_bytes=64, offset=(SCALE_AT - 1) * KB)
-        halves = [slice(h * S // 2, (h + 1) * S // 2) for h in range(2)]
-        for h, cols in enumerate(halves):
-            nc.vector.tensor_copy(x_codes[:, cols], word_win[:].bitcast(U32).indirect(offs_sb[:, h * 16 : (h + 1) * 16]))
+        nc.vector.tensor_copy(x_codes[:], word_win[:].bitcast(U32).indirect(offs_sb[:]))
 
         for i, t in enumerate(ORDER):
             rows = slice(t * P, (t + 1) * P)
             y[t] = []
-            for cols in halves if i == 0 else [slice(0, S)]:
+            for cols in [slice(0, S)]:
                 bank = psum.tile([P, cols.stop - cols.start], F32, name="y%d_%d" % (t, cols.start))
                 nc.tensor.matmul_mx(
                     out=bank[:],
@@ -186,8 +184,9 @@ def tile_picked_adagr8_none_po_kernel(
                 nc.scalar.copy(out_bf[:, :, t], par_win[t][:])
 
         last = ORDER[-1]
-        load_par(2)
-        fetch_par(2)
+        for i in (2, 3):
+            load_par(i)
+            fetch_par(i)
         square(0)
         square(1)
         copy_y(0)
@@ -208,7 +207,6 @@ def tile_picked_adagr8_none_po_kernel(
         load_par(0)
         fetch_par(0)
         load_par(1)
-        load_par(3)
         product(1)
         tot_last = arena.tile([P, S], F32, name="tot_last", offset=TOT_LAST_AT * KB)
         nc.gpsimd.tensor_tensor(tot_last[:], ssq_last[:], y2[last][:], ALU.add)
@@ -219,7 +217,6 @@ def tile_picked_adagr8_none_po_kernel(
         put(1)
         product(2)
         product(3)
-        fetch_par(3)
         put(2)
         put(3)
 

@@ -29,9 +29,9 @@ PAR_AT = (84, 40, 10, 14)
 SSQ_AT = (18, 22, 78, 26)
 SQUARE_AT = (64, 62, 18, 20)
 Y_AT = (60, 22, 24, 62)
-STEP_AT = (90, 89, 90, 87)
+STEP_AT = (90, 89, 88, 90)
 TOT_LAST_AT = 91
-OUT_BF_AT = 92
+OUT_BF_AT = (96, 92)
 GOT_AT = (52, 54, 56, 58)
 
 
@@ -181,9 +181,16 @@ def tile_picked_adagr8_none_po_kernel(
                 nc.vector.tensor_tensor(par_win[t][:].indirect(ent_sb[:]), par_got[t][:], step[t][:], ALU.add)
             nc.sync.dma_start(out_rows[:, t, :], par_win[t][:])
             if i + 1 < PACK:
-                nc.scalar.copy(out_bf[:, :, t], par_win[t][:])
+                for h in range(2):
+                    nc.scalar.copy(out_bf[h][:, :, t], par_win[t][:, h * uh : (h + 1) * uh])
+                    if i == 0 and h == 0:
+                        root(last, tot_last)
 
         last = ORDER[-1]
+        uh = U // 2
+        out_bf = [
+            arena.tile([P, uh, PACK], BF16, name="out_bf%d" % h, align_bytes=64, offset=OUT_BF_AT[h] * KB) for h in range(2)
+        ]
         for i in (2, 3):
             load_par(i)
             fetch_par(i)
@@ -207,11 +214,9 @@ def tile_picked_adagr8_none_po_kernel(
         load_par(0)
         fetch_par(0)
         load_par(1)
-        product(1)
         tot_last = arena.tile([P, S], F32, name="tot_last", offset=TOT_LAST_AT * KB)
         nc.gpsimd.tensor_tensor(tot_last[:], ssq_last[:], y2[last][:], ALU.add)
-        root(last, tot_last)
-        out_bf = arena.tile([P, U, PACK], BF16, name="out_bf", align_bytes=64, offset=OUT_BF_AT * KB)
+        product(1)
         put(0)
         fetch_par(1)
         put(1)
@@ -222,10 +227,14 @@ def tile_picked_adagr8_none_po_kernel(
 
         oc = U // OUT_CHUNKS
         chunks = [slice(c * oc, (c + 1) * oc) for c in range(OUT_CHUNKS)]
+
+        def staged(cols):
+            return out_bf[cols.start // uh][:, cols.start % uh : cols.start % uh + oc, :]
+
         for cols in chunks[OUT_CHUNKS // 2 :]:
-            nc.scalar.copy(out_bf[:, cols, last], par_win[last][:, cols])
+            nc.scalar.copy(staged(cols)[:, :, last], par_win[last][:, cols])
         for cols in chunks[: OUT_CHUNKS // 2]:
-            nc.vector.tensor_copy(out_bf[:, cols, last], par_win[last][:, cols])
+            nc.vector.tensor_copy(staged(cols)[:, :, last], par_win[last][:, cols])
 
         out_codes = held.tile([P, U], U32, name="out_codes", align_bytes=64)
         out_scale = held.tile([P, U], U8, name="out_scale", align_bytes=64)
@@ -235,7 +244,7 @@ def tile_picked_adagr8_none_po_kernel(
             nc.vector.quantize_mx(
                 out=out_codes[:, cols].bitcast(FP8X4),
                 scales=out_scale[:, cols],
-                in_=out_bf[:, cols, :].rearrange("p u t -> p (u t)"),
+                in_=staged(cols).rearrange("p u t -> p (u t)"),
             )
             if c > 0:
                 nc.sync.dma_start(words_hbm[:, stored : cols.stop], out_codes[:, stored : cols.stop].bitcast(I32))

@@ -18,20 +18,22 @@ ACT = mybir.ActivationFunctionType
 P = 128
 PACK = 4
 W_CHUNKS = 2
-OUT_CHUNKS = 4
-ORDER = (2, 0, 1, 3)
+ORDER = (2, 0, 3, 1)
+LOW_CHUNKS = (256, 256, 128)
+HIGH_CHUNKS = (256, 128)
+VECTOR_COLS = 576
 KB = 1024
 W_RAW_AT = (48, 16)
 W_BF_AT = 24
 WORD_AT = 78
 SCALE_AT = 44
-PAR_AT = (84, 40, 10, 14)
-SSQ_AT = (18, 22, 78, 26)
-SQUARE_AT = (64, 62, 18, 20)
-Y_AT = (60, 22, 24, 62)
-STEP_AT = (90, 89, 88, 90)
-TOT_LAST_AT = 91
-OUT_BF_AT = (96, 92)
+PAR_AT = (78, 40, 10, 26)
+SSQ_AT = (14, 18, 82, 22)
+SQUARE_AT = (60, 72, 14, 16)
+Y_AT = (70, 63, 65, 18)
+TOT_AT = (64, 74, 62, 91)
+STEP_AT = (90, 89, 98, 82)
+OUT_BF_AT = (92, 60)
 GOT_AT = (52, 54, 56, 58)
 
 
@@ -103,12 +105,14 @@ def tile_picked_adagr8_none_po_kernel(
         )
 
         x_codes = arena.tile([P, S], U32, name="x_codes", align_bytes=64, offset=(SCALE_AT - 1) * KB)
-        nc.vector.tensor_copy(x_codes[:], word_win[:].bitcast(U32).indirect(offs_sb[:]))
+        halves = [slice(h * S // 2, (h + 1) * S // 2) for h in range(2)]
+        for h, cols in enumerate(halves):
+            nc.vector.tensor_copy(x_codes[:, cols], word_win[:].bitcast(U32).indirect(offs_sb[:, h * 16 : (h + 1) * 16]))
 
         for i, t in enumerate(ORDER):
             rows = slice(t * P, (t + 1) * P)
             y[t] = []
-            for cols in [slice(0, S)]:
+            for cols in halves if i == 0 else [slice(0, S)]:
                 bank = psum.tile([P, cols.stop - cols.start], F32, name="y%d_%d" % (t, cols.start))
                 nc.tensor.matmul_mx(
                     out=bank[:],
@@ -164,7 +168,7 @@ def tile_picked_adagr8_none_po_kernel(
 
         def fetch_ssq(i):
             t = ORDER[i]
-            tot = held.tile([P, S], F32, name="tot%d" % t)
+            tot = arena.tile([P, S], F32, name="tot%d" % t, offset=TOT_AT[i] * KB)
             nc.vector.tensor_tensor(tot[:], ssq_win[t][:].indirect(ent_sb[:]), y2[t][:], ALU.add)
             root(t, tot)
 
@@ -180,62 +184,74 @@ def tile_picked_adagr8_none_po_kernel(
             else:
                 nc.vector.tensor_tensor(par_win[t][:].indirect(ent_sb[:]), par_got[t][:], step[t][:], ALU.add)
             nc.sync.dma_start(out_rows[:, t, :], par_win[t][:])
-            if i + 1 < PACK:
-                for h in range(2):
-                    nc.scalar.copy(out_bf[h][:, :, t], par_win[t][:, h * uh : (h + 1) * uh])
-                    if i == 0 and h == 0:
-                        root(last, tot_last)
+
+        low = sum(LOW_CHUNKS)
+        parts = [slice(0, low), slice(low, U)]
+        out_bf = {}
+
+        def round_part(i, h):
+            t = ORDER[i]
+            if i == 0:
+                width = parts[h].stop - parts[h].start
+                out_bf[h] = arena.tile([P, width, PACK], BF16, name="out_bf%d" % h, align_bytes=64, offset=OUT_BF_AT[h] * KB)
+            nc.scalar.copy(out_bf[h][:, :, t], par_win[t][:, parts[h]])
 
         last = ORDER[-1]
-        uh = U // 2
-        out_bf = [
-            arena.tile([P, uh, PACK], BF16, name="out_bf%d" % h, align_bytes=64, offset=OUT_BF_AT[h] * KB) for h in range(2)
-        ]
-        for i in (2, 3):
-            load_par(i)
-            fetch_par(i)
+        load_par(2)
+        fetch_par(2)
         square(0)
         square(1)
         copy_y(0)
-        load_ssq(0)
-        fetch_ssq(0)
-        load_ssq(1)
-        fetch_ssq(1)
-        square(2)
-        square(3)
+        for i in range(2):
+            load_ssq(i)
+            fetch_ssq(i)
+        for i in range(2, PACK):
+            square(i)
         load_ssq(3)
         ssq_last = held.tile([P, S], F32, name="ssq_last")
         nc.vector.tensor_copy(ssq_last[:], ssq_win[last][:].indirect(ent_sb[:]))
         product(0)
-        load_ssq(2)
-        fetch_ssq(2)
         for i in range(1, PACK):
             copy_y(i)
+        load_par(3)
+        fetch_par(3)
         load_par(0)
         fetch_par(0)
-        load_par(1)
-        tot_last = arena.tile([P, S], F32, name="tot_last", offset=TOT_LAST_AT * KB)
+        put(0)
+        tot_last = arena.tile([P, S], F32, name="tot_last", offset=TOT_AT[3] * KB)
         nc.gpsimd.tensor_tensor(tot_last[:], ssq_last[:], y2[last][:], ALU.add)
         product(1)
-        put(0)
+        root(last, tot_last)
+        round_part(0, 0)
+        load_ssq(2)
+        load_par(1)
         fetch_par(1)
+        fetch_ssq(2)
         put(1)
-        product(2)
         product(3)
+        product(2)
+        round_part(0, 1)
+        for i in (1, 3):
+            if i > 1:
+                put(i)
+            for h in range(2):
+                round_part(i, h)
         put(2)
-        put(3)
-
-        oc = U // OUT_CHUNKS
-        chunks = [slice(c * oc, (c + 1) * oc) for c in range(OUT_CHUNKS)]
+        last = ORDER[2]
 
         def staged(cols):
-            return out_bf[cols.start // uh][:, cols.start % uh : cols.start % uh + oc, :]
+            h = 0 if cols.start < low else 1
+            return out_bf[h][:, cols.start - parts[h].start : cols.stop - parts[h].start, :]
 
-        for cols in chunks[OUT_CHUNKS // 2 :]:
+        for cols in (slice(VECTOR_COLS, low), slice(low, low + 256), slice(low + 256, U)):
             nc.scalar.copy(staged(cols)[:, :, last], par_win[last][:, cols])
-        for cols in chunks[: OUT_CHUNKS // 2]:
+        for cols in (slice(0, 256), slice(256, VECTOR_COLS)):
             nc.vector.tensor_copy(staged(cols)[:, :, last], par_win[last][:, cols])
 
+        chunks = []
+        for width in LOW_CHUNKS + HIGH_CHUNKS:
+            start = chunks[-1].stop if chunks else 0
+            chunks.append(slice(start, start + width))
         out_codes = held.tile([P, U], U32, name="out_codes", align_bytes=64)
         out_scale = held.tile([P, U], U8, name="out_scale", align_bytes=64)
         words_hbm = out_1[0].rearrange("p n t -> p (n t)").bitcast(I32)
@@ -246,7 +262,7 @@ def tile_picked_adagr8_none_po_kernel(
                 scales=out_scale[:, cols],
                 in_=staged(cols).rearrange("p u t -> p (u t)"),
             )
-            if c > 0:
+            if c in (1, 3, 4):
                 nc.sync.dma_start(words_hbm[:, stored : cols.stop], out_codes[:, stored : cols.stop].bitcast(I32))
                 stored = cols.stop
         for q in range(4):

@@ -17,24 +17,28 @@ ACT = mybir.ActivationFunctionType
 
 P = 128
 PACK = 4
-W_CHUNKS = 2
-ORDER = (2, 0, 3, 1)
-LOW_CHUNKS = (256, 256, 128)
-HIGH_CHUNKS = (256, 128)
-VECTOR_COLS = 576
+GROUP = 16
+QUAD = 32
+OUT_CHUNKS = 4
+
+A, B, C, D = range(PACK)
+ROW = (2, 0, 1, 3)
+FUSED_PAR = (A, B)
+
 KB = 1024
 W_RAW_AT = (48, 16)
 W_BF_AT = 24
 WORD_AT = 78
 SCALE_AT = 44
-PAR_AT = (78, 40, 10, 26)
+CODES_AT = 43
+PAR_AT = (26, 78, 10, 40)
 SSQ_AT = (14, 18, 82, 22)
 SQUARE_AT = (60, 72, 14, 16)
 Y_AT = (70, 63, 65, 18)
-TOT_AT = (64, 74, 62, 91)
-STEP_AT = (90, 89, 98, 82)
-OUT_BF_AT = (92, 60)
-GOT_AT = (52, 54, 56, 58)
+TOTAL_AT = (64, 74, 62, 91)
+STEP_AT = (90, 89, 98, 63)
+GOT_AT = (52, 54, 56, 82)
+ROUNDED_AT = (92, 59)
 
 
 def tile_picked_adagr8_none_po_kernel(
@@ -47,27 +51,26 @@ def tile_picked_adagr8_none_po_kernel(
         arena = ctx.enter_context(tc.tile_pool(name="arena", bufs=1))
         psum = ctx.enter_context(tc.psum_pool(name="psum", bufs=1))
 
-        offs_sb = lists.tile([P, S // 16], U16, name="offs_sb")
-        ent_sb = lists.tile([P, S // 16], U16, name="ent_sb")
+        offs_sb = lists.tile([P, S // GROUP], U16, name="offs_sb")
+        ent_sb = lists.tile([P, S // GROUP], U16, name="ent_sb")
 
-        wc = N // W_CHUNKS
+        w_half = N // 2
         w_rows = w1.rearrange("(p j) c -> p j c", j=PACK)
-        w_raw = [
-            arena.tile([P, PACK, wc], F32, name="w_raw%d" % h, offset=W_RAW_AT[h] * KB) for h in range(W_CHUNKS)
-        ]
-        nc.sync.dma_start(w_raw[0][:], w_rows[:, :, :wc])
+        w_raw = [arena.tile([P, PACK, w_half], F32, name="w_raw%d" % h, offset=W_RAW_AT[h] * KB) for h in range(2)]
+        nc.sync.dma_start(w_raw[0][:], w_rows[:, :, :w_half])
         nc.sync.dma_start(offs_sb[:], offs)
 
         scale_win = arena.tile([P, T], U8, name="scale_win", align_bytes=64, offset=SCALE_AT * KB)
         nc.vector.memset(scale_win[:].bitcast(I32), 0)
         for e in range(2):
-            nc.sync.dma_start(scale_win[e:P:16, :].bitcast(I32), x_scales[0, e:16:2, :].bitcast(I32))
+            nc.sync.dma_start(scale_win[e:P:GROUP, :].bitcast(I32), x_scales[0, e:16:2, :].bitcast(I32))
+
         warm = held.tile([P, 1], F32, name="warm")
         warm_out = held.tile([P, 1], F32, name="warm_out")
         nc.gpsimd.memset(warm[:], 1.0)
         nc.scalar.activation(warm_out[:], warm[:], ACT.Abs_reciprocal_sqrt)
 
-        nc.sync.dma_start(w_raw[1][:], w_rows[:, :, wc:])
+        nc.sync.dma_start(w_raw[1][:], w_rows[:, :, w_half:])
         word_win = arena.tile([P, T], I32, name="word_win", align_bytes=64, offset=WORD_AT * KB)
         nc.sync.dma_start(word_win[:], x_words[0].rearrange("p n t -> p (n t)").bitcast(I32))
         nc.sync.dma_start(ent_sb[:], ent)
@@ -81,177 +84,166 @@ def tile_picked_adagr8_none_po_kernel(
         x_scale = held.tile([P, S], U8, name="x_scale", align_bytes=64)
         nc.vector.tensor_copy(x_scale[:].bitcast(I32), scale_got[:].bitcast(I32))
         for e in range(2):
-            nc.scalar.dma_start(x_scale[2 + e : P : 32, :].bitcast(I32), scale_got[16 + e : P : 32, :].bitcast(I32))
+            nc.scalar.dma_start(
+                x_scale[2 + e : P : QUAD, :].bitcast(I32), scale_got[GROUP + e : P : QUAD, :].bitcast(I32)
+            )
 
         w_bf = arena.tile([P, PACK, P, PACK], BF16, name="w_bf", align_bytes=64, offset=W_BF_AT * KB)
-        mc = wc // PACK
-        for h in range(W_CHUNKS):
-            dst = w_bf[:, :, h * mc : (h + 1) * mc, :].rearrange("p t m j -> p m t j")
-            src = w_raw[h][:].rearrange("p j (m t) -> p m t j", t=PACK)
-            if h == 0:
-                nc.scalar.copy(dst, src)
-            else:
-                nc.vector.tensor_copy(dst, src)
+        m_half = w_half // PACK
+        for h, copy in enumerate((nc.scalar.copy, nc.vector.tensor_copy)):
+            copy(
+                w_bf[:, :, h * m_half : (h + 1) * m_half, :].rearrange("p t m j -> p m t j"),
+                w_raw[h][:].rearrange("p j (m t) -> p m t j", t=PACK),
+            )
         w_codes = held.tile([P, N], U32, name="w_codes", align_bytes=64)
         w_scale = held.tile([P, N], U8, name="w_scale", align_bytes=64)
-
-
-        y = {}
-        y2 = {}
         nc.vector.quantize_mx(
             out=w_codes[:].bitcast(FP8X4),
             scales=w_scale[:],
             in_=w_bf[:].rearrange("p t m j -> p (t m j)"),
         )
 
-        x_codes = arena.tile([P, S], U32, name="x_codes", align_bytes=64, offset=(SCALE_AT - 1) * KB)
-        halves = [slice(h * S // 2, (h + 1) * S // 2) for h in range(2)]
-        for h, cols in enumerate(halves):
-            nc.vector.tensor_copy(x_codes[:, cols], word_win[:].bitcast(U32).indirect(offs_sb[:, h * 16 : (h + 1) * 16]))
+        x_codes = arena.tile([P, S], U32, name="x_codes", align_bytes=64, offset=CODES_AT * KB)
+        entry_halves = [slice(h * S // 2, (h + 1) * S // 2) for h in range(2)]
+        for cols in entry_halves:
+            picks = offs_sb[:, cols.start // GROUP : cols.stop // GROUP]
+            nc.vector.tensor_copy(x_codes[:, cols], word_win[:].bitcast(U32).indirect(picks))
 
-        for i, t in enumerate(ORDER):
-            rows = slice(t * P, (t + 1) * P)
-            y[t] = []
-            for cols in halves if i == 0 else [slice(0, S)]:
+        y_banks = {}
+        for i, t in enumerate(ROW):
+            w_cols = slice(t * P, (t + 1) * P)
+            y_banks[i] = []
+            for cols in entry_halves if i == A else [slice(0, S)]:
                 bank = psum.tile([P, cols.stop - cols.start], F32, name="y%d_%d" % (t, cols.start))
                 nc.tensor.matmul_mx(
                     out=bank[:],
-                    lhsT=w_codes[:, rows].bitcast(FP8X4),
-                    lhsT_scale=w_scale[:, rows],
+                    lhsT=w_codes[:, w_cols].bitcast(FP8X4),
+                    lhsT_scale=w_scale[:, w_cols],
                     rhs=x_codes[:, cols].bitcast(FP8X4),
                     rhs_scale=x_scale[:, cols],
                     start=True,
                     stop=True,
                 )
-                y[t].append((cols, bank))
+                y_banks[i].append((cols, bank))
 
+        y_sq = {}
         y_sb = {}
         par_win = {}
         par_got = {}
         ssq_win = {}
-        rs = {}
+        inv_root = {}
         step = {}
+        rounded = {}
+        col_half = U // 2
 
         def square(i):
-            t = ORDER[i]
-            y2[t] = arena.tile([P, S], F32, name="y2_%d" % t, offset=SQUARE_AT[i] * KB)
-            for cols, bank in y[t]:
-                nc.scalar.activation(y2[t][:, cols], bank[:], ACT.Square)
+            y_sq[i] = arena.tile([P, S], F32, name="y_sq%d" % i, offset=SQUARE_AT[i] * KB)
+            for cols, bank in y_banks[i]:
+                nc.scalar.activation(y_sq[i][:, cols], bank[:], ACT.Square)
 
         def copy_y(i):
-            t = ORDER[i]
-            y_sb[t] = arena.tile([P, S], F32, name="y_sb%d" % t, offset=Y_AT[i] * KB)
-            for cols, bank in y[t]:
-                nc.scalar.activation(y_sb[t][:, cols], bank[:], ACT.Copy, scale=1.0 if i < 2 else -1.0)
+            y_sb[i] = arena.tile([P, S], F32, name="y_sb%d" % i, offset=Y_AT[i] * KB)
+            for cols, bank in y_banks[i]:
+                nc.scalar.activation(y_sb[i][:, cols], bank[:], ACT.Copy, scale=1.0 if i in FUSED_PAR else -1.0)
 
         def load_par(i):
-            t = ORDER[i]
-            par_win[t] = arena.tile([P, U], F32, name="par_win%d" % t, offset=PAR_AT[i] * KB)
-            nc.sync.dma_start(par_win[t][:], par_rows[:, t, :])
+            par_win[i] = arena.tile([P, U], F32, name="par_win%d" % i, offset=PAR_AT[i] * KB)
+            nc.sync.dma_start(par_win[i][:], par_rows[:, ROW[i], :])
 
         def load_ssq(i):
-            t = ORDER[i]
-            ssq_win[t] = arena.tile([P, U], F32, name="ssq_win%d" % t, offset=SSQ_AT[i] * KB)
-            nc.sync.dma_start(ssq_win[t][:], ssq_rows[:, t, :])
+            ssq_win[i] = arena.tile([P, U], F32, name="ssq_win%d" % i, offset=SSQ_AT[i] * KB)
+            nc.sync.dma_start(ssq_win[i][:], ssq_rows[:, ROW[i], :])
 
-        def fetch_par(i):
-            t = ORDER[i]
-            par_got[t] = arena.tile([P, S], F32, name="par_got%d" % t, offset=GOT_AT[i] * KB)
-            if i < 2:
-                nc.vector.tensor_tensor(par_got[t][:], par_win[t][:].indirect(ent_sb[:]), step[t][:], ALU.subtract)
+        def gather_par(i):
+            par_got[i] = arena.tile([P, S], F32, name="par_got%d" % i, offset=GOT_AT[i] * KB)
+            if i in FUSED_PAR:
+                nc.vector.tensor_tensor(par_got[i][:], par_win[i][:].indirect(ent_sb[:]), step[i][:], ALU.subtract)
             else:
-                nc.vector.tensor_copy(par_got[t][:], par_win[t][:].indirect(ent_sb[:]))
+                nc.vector.tensor_copy(par_got[i][:], par_win[i][:].indirect(ent_sb[:]))
 
-        def root(t, tot):
-            rs[t] = held.tile([P, S], F32, name="rs%d" % t)
-            nc.scalar.activation(rs[t][:], tot[:], ACT.Abs_reciprocal_sqrt)
+        def root(i, total):
+            inv_root[i] = held.tile([P, S], F32, name="inv_root%d" % i)
+            nc.scalar.activation(inv_root[i][:], total[:], ACT.Abs_reciprocal_sqrt)
 
-        def fetch_ssq(i):
-            t = ORDER[i]
-            tot = arena.tile([P, S], F32, name="tot%d" % t, offset=TOT_AT[i] * KB)
-            nc.vector.tensor_tensor(tot[:], ssq_win[t][:].indirect(ent_sb[:]), y2[t][:], ALU.add)
-            root(t, tot)
+        def gather_ssq_and_root(i):
+            total = arena.tile([P, S], F32, name="total%d" % i, offset=TOTAL_AT[i] * KB)
+            nc.vector.tensor_tensor(total[:], ssq_win[i][:].indirect(ent_sb[:]), y_sq[i][:], ALU.add)
+            root(i, total)
 
         def product(i):
-            t = ORDER[i]
-            step[t] = arena.tile([P, S], F32, name="step%d" % t, offset=STEP_AT[i] * KB)
-            nc.gpsimd.tensor_tensor(step[t][:], y_sb[t][:], rs[t][:], ALU.mult)
+            step[i] = arena.tile([P, S], F32, name="step%d" % i, offset=STEP_AT[i] * KB)
+            nc.gpsimd.tensor_tensor(step[i][:], y_sb[i][:], inv_root[i][:], ALU.mult)
 
-        def put(i):
-            t = ORDER[i]
-            if i < 2:
-                nc.vector.tensor_copy(par_win[t][:].indirect(ent_sb[:]), par_got[t][:])
+        def scatter_and_store(i):
+            if i in FUSED_PAR:
+                nc.vector.tensor_copy(par_win[i][:].indirect(ent_sb[:]), par_got[i][:])
             else:
-                nc.vector.tensor_tensor(par_win[t][:].indirect(ent_sb[:]), par_got[t][:], step[t][:], ALU.add)
-            nc.sync.dma_start(out_rows[:, t, :], par_win[t][:])
+                nc.vector.tensor_tensor(par_win[i][:].indirect(ent_sb[:]), par_got[i][:], step[i][:], ALU.add)
+            nc.sync.dma_start(out_rows[:, ROW[i], :], par_win[i][:])
 
-        low = sum(LOW_CHUNKS)
-        parts = [slice(0, low), slice(low, U)]
-        out_bf = {}
+        def round_half(i, h):
+            if i == A:
+                rounded[h] = arena.tile(
+                    [P, col_half, PACK], BF16, name="rounded%d" % h, align_bytes=64, offset=ROUNDED_AT[h] * KB
+                )
+            nc.scalar.copy(rounded[h][:, :, ROW[i]], par_win[i][:, h * col_half : (h + 1) * col_half])
 
-        def round_part(i, h):
-            t = ORDER[i]
-            if i == 0:
-                width = parts[h].stop - parts[h].start
-                out_bf[h] = arena.tile([P, width, PACK], BF16, name="out_bf%d" % h, align_bytes=64, offset=OUT_BF_AT[h] * KB)
-            nc.scalar.copy(out_bf[h][:, :, t], par_win[t][:, parts[h]])
-
-        last = ORDER[-1]
-        load_par(2)
-        fetch_par(2)
-        square(0)
-        square(1)
-        copy_y(0)
-        for i in range(2):
+        load_par(C)
+        gather_par(C)
+        square(A)
+        square(B)
+        copy_y(A)
+        for i in (A, B):
             load_ssq(i)
-            fetch_ssq(i)
-        for i in range(2, PACK):
-            square(i)
-        load_ssq(3)
-        ssq_last = held.tile([P, S], F32, name="ssq_last")
-        nc.vector.tensor_copy(ssq_last[:], ssq_win[last][:].indirect(ent_sb[:]))
-        product(0)
-        for i in range(1, PACK):
+            gather_ssq_and_root(i)
+        square(C)
+        square(D)
+
+        load_ssq(D)
+        ssq_got = held.tile([P, S], F32, name="ssq_got")
+        nc.vector.tensor_copy(ssq_got[:], ssq_win[D][:].indirect(ent_sb[:]))
+        product(A)
+        for i in (B, C, D):
             copy_y(i)
-        load_par(3)
-        fetch_par(3)
-        load_par(0)
-        fetch_par(0)
-        put(0)
-        tot_last = arena.tile([P, S], F32, name="tot_last", offset=TOT_AT[3] * KB)
-        nc.gpsimd.tensor_tensor(tot_last[:], ssq_last[:], y2[last][:], ALU.add)
-        product(1)
-        root(last, tot_last)
-        round_part(0, 0)
-        load_ssq(2)
-        load_par(1)
-        fetch_par(1)
-        fetch_ssq(2)
-        put(1)
-        product(3)
-        product(2)
-        round_part(0, 1)
-        for i in (1, 3):
-            if i > 1:
-                put(i)
-            for h in range(2):
-                round_part(i, h)
-        put(2)
-        last = ORDER[2]
 
-        def staged(cols):
-            h = 0 if cols.start < low else 1
-            return out_bf[h][:, cols.start - parts[h].start : cols.stop - parts[h].start, :]
+        load_par(A)
+        gather_par(A)
+        scatter_and_store(A)
+        total_d = arena.tile([P, S], F32, name="total_d", offset=TOTAL_AT[D] * KB)
+        nc.gpsimd.tensor_tensor(total_d[:], ssq_got[:], y_sq[D][:], ALU.add)
+        product(B)
+        root(D, total_d)
+        round_half(A, 0)
 
-        for cols in (slice(VECTOR_COLS, low), slice(low, low + 256), slice(low + 256, U)):
-            nc.scalar.copy(staged(cols)[:, :, last], par_win[last][:, cols])
-        for cols in (slice(0, 256), slice(256, VECTOR_COLS)):
-            nc.vector.tensor_copy(staged(cols)[:, :, last], par_win[last][:, cols])
+        load_ssq(C)
+        load_par(B)
+        load_par(D)
+        gather_par(B)
+        gather_ssq_and_root(C)
+        scatter_and_store(B)
+        gather_par(D)
+        product(C)
+        product(D)
+        round_half(A, 1)
+        for h in range(2):
+            round_half(B, h)
+        scatter_and_store(C)
+        for h in range(2):
+            round_half(C, h)
+        scatter_and_store(D)
 
-        chunks = []
-        for width in LOW_CHUNKS + HIGH_CHUNKS:
-            start = chunks[-1].stop if chunks else 0
-            chunks.append(slice(start, start + width))
+        width = U // OUT_CHUNKS
+        chunks = [slice(c * width, (c + 1) * width) for c in range(OUT_CHUNKS)]
+
+        def rounded_chunk(cols):
+            start = cols.start % col_half
+            return rounded[cols.start // col_half][:, start : start + width, :]
+
+        for cols in chunks[OUT_CHUNKS // 2 :]:
+            nc.scalar.copy(rounded_chunk(cols)[:, :, ROW[D]], par_win[D][:, cols])
+        for cols in chunks[: OUT_CHUNKS // 2]:
+            nc.vector.tensor_copy(rounded_chunk(cols)[:, :, ROW[D]], par_win[D][:, cols])
+
         out_codes = held.tile([P, U], U32, name="out_codes", align_bytes=64)
         out_scale = held.tile([P, U], U8, name="out_scale", align_bytes=64)
         words_hbm = out_1[0].rearrange("p n t -> p (n t)").bitcast(I32)
@@ -260,11 +252,13 @@ def tile_picked_adagr8_none_po_kernel(
             nc.vector.quantize_mx(
                 out=out_codes[:, cols].bitcast(FP8X4),
                 scales=out_scale[:, cols],
-                in_=staged(cols).rearrange("p u t -> p (u t)"),
+                in_=rounded_chunk(cols).rearrange("p u t -> p (u t)"),
             )
-            if c in (1, 3, 4):
+            if c > 0:
                 nc.sync.dma_start(words_hbm[:, stored : cols.stop], out_codes[:, stored : cols.stop].bitcast(I32))
                 stored = cols.stop
-        for q in range(4):
-            eng = nc.scalar if q % 2 == 0 else nc.sync
-            eng.dma_start(out_2[0, 4 * q : 4 * q + 4, :].bitcast(I32), out_scale[32 * q : 32 * q + 4, :].bitcast(I32))
+        for q in range(P // QUAD):
+            queue = nc.scalar if q % 2 == 0 else nc.sync
+            queue.dma_start(
+                out_2[0, 4 * q : 4 * q + 4, :].bitcast(I32), out_scale[QUAD * q : QUAD * q + 4, :].bitcast(I32)
+            )

@@ -19,7 +19,6 @@ P = 128
 PACK = 4
 GROUP = 16
 QUAD = 32
-OUT_CHUNKS = 4
 
 A, B, C, D = range(PACK)
 ROW = (2, 0, 1, 3)
@@ -136,6 +135,12 @@ def tile_picked_adagr8_none_po_kernel(
         rounded = {}
         col_half = U // 2
 
+        def pieces(i):
+            return entry_halves if i == A else [slice(0, S)]
+
+        def entries(cols):
+            return ent_sb[:, cols.start // GROUP : cols.stop // GROUP]
+
         def square(i):
             y_sq[i] = arena.tile([P, S], F32, name="y_sq%d" % i, offset=SQUARE_AT[i] * KB)
             for cols, bank in y_banks[i]:
@@ -157,7 +162,10 @@ def tile_picked_adagr8_none_po_kernel(
         def gather_par(i):
             par_got[i] = arena.tile([P, S], F32, name="par_got%d" % i, offset=GOT_AT[i] * KB)
             if i in FUSED_PAR:
-                nc.vector.tensor_tensor(par_got[i][:], par_win[i][:].indirect(ent_sb[:]), step[i][:], ALU.subtract)
+                for cols in pieces(i):
+                    nc.vector.tensor_tensor(
+                        par_got[i][:, cols], par_win[i][:].indirect(entries(cols)), step[i][:, cols], ALU.subtract
+                    )
             else:
                 nc.vector.tensor_copy(par_got[i][:], par_win[i][:].indirect(ent_sb[:]))
 
@@ -167,12 +175,14 @@ def tile_picked_adagr8_none_po_kernel(
 
         def gather_ssq_and_root(i):
             total = arena.tile([P, S], F32, name="total%d" % i, offset=TOTAL_AT[i] * KB)
-            nc.vector.tensor_tensor(total[:], ssq_win[i][:].indirect(ent_sb[:]), y_sq[i][:], ALU.add)
+            for cols in pieces(i):
+                nc.vector.tensor_tensor(total[:, cols], ssq_win[i][:].indirect(entries(cols)), y_sq[i][:, cols], ALU.add)
             root(i, total)
 
         def product(i):
             step[i] = arena.tile([P, S], F32, name="step%d" % i, offset=STEP_AT[i] * KB)
-            nc.gpsimd.tensor_tensor(step[i][:], y_sb[i][:], inv_root[i][:], ALU.mult)
+            for cols in pieces(i):
+                nc.gpsimd.tensor_tensor(step[i][:, cols], y_sb[i][:, cols], inv_root[i][:, cols], ALU.mult)
 
         def scatter_and_store(i):
             if i in FUSED_PAR:
@@ -232,16 +242,16 @@ def tile_picked_adagr8_none_po_kernel(
             round_half(C, h)
         scatter_and_store(D)
 
-        width = U // OUT_CHUNKS
-        chunks = [slice(c * width, (c + 1) * width) for c in range(OUT_CHUNKS)]
+        edges = (0, 256, 512, 768, 896, 1024)
+        chunks = [slice(a, b) for a, b in zip(edges, edges[1:])]
 
         def rounded_chunk(cols):
             start = cols.start % col_half
-            return rounded[cols.start // col_half][:, start : start + width, :]
+            return rounded[cols.start // col_half][:, start : start + cols.stop - cols.start, :]
 
-        for cols in chunks[OUT_CHUNKS // 2 :]:
+        for cols in chunks[2:]:
             nc.scalar.copy(rounded_chunk(cols)[:, :, ROW[D]], par_win[D][:, cols])
-        for cols in chunks[: OUT_CHUNKS // 2]:
+        for cols in chunks[:2]:
             nc.vector.tensor_copy(rounded_chunk(cols)[:, :, ROW[D]], par_win[D][:, cols])
 
         out_codes = held.tile([P, U], U32, name="out_codes", align_bytes=64)
@@ -254,7 +264,7 @@ def tile_picked_adagr8_none_po_kernel(
                 scales=out_scale[:, cols],
                 in_=rounded_chunk(cols).rearrange("p u t -> p (u t)"),
             )
-            if c > 0:
+            if c not in (0, 2):
                 nc.sync.dma_start(words_hbm[:, stored : cols.stop], out_codes[:, stored : cols.stop].bitcast(I32))
                 stored = cols.stop
         for q in range(P // QUAD):

@@ -30,14 +30,14 @@ W_BF_AT = 24
 WORD_AT = 78
 SCALE_AT = 44
 CODES_AT = 43
-PAR_AT = (26, 78, 10, 40)
-SSQ_AT = (14, 18, 82, 22)
+PAR_AT = (26, 78, 150, 40)
+SSQ_AT = (14, 18, 22, 82)
 SQUARE_AT = (60, 72, 14, 16)
 Y_AT = (70, 63, 65, 18)
-TOTAL_AT = (64, 74, 62, 91)
-STEP_AT = (90, 89, 98, 63)
+TOTAL_AT = (64, 74, 91, 13)
+STEP_AT = (90, 14, 16, 98)
 GOT_AT = (52, 54, 56, 82)
-ROUNDED_AT = (92, 59)
+ROUNDED_AT = (92, 88)
 
 
 def tile_picked_adagr8_none_po_kernel(
@@ -136,7 +136,7 @@ def tile_picked_adagr8_none_po_kernel(
         col_half = U // 2
 
         def pieces(i):
-            return entry_halves if i == A else [slice(0, S)]
+            return entry_halves if i in FUSED_PAR else [slice(0, S)]
 
         def entries(cols):
             return ent_sb[:, cols.start // GROUP : cols.stop // GROUP]
@@ -164,7 +164,7 @@ def tile_picked_adagr8_none_po_kernel(
             if i in FUSED_PAR:
                 for cols in pieces(i):
                     nc.vector.tensor_tensor(
-                        par_got[i][:, cols], par_win[i][:].indirect(entries(cols)), step[i][:, cols], ALU.subtract
+                        par_got[i][:, cols], par_win[i][:].indirect(entries(cols)), step[i, cols.start][:], ALU.subtract
                     )
             else:
                 nc.vector.tensor_copy(par_got[i][:], par_win[i][:].indirect(ent_sb[:]))
@@ -175,20 +175,22 @@ def tile_picked_adagr8_none_po_kernel(
 
         def gather_ssq_and_root(i):
             total = arena.tile([P, S], F32, name="total%d" % i, offset=TOTAL_AT[i] * KB)
-            for cols in pieces(i):
+            for cols in entry_halves if i == A else [slice(0, S)]:
                 nc.vector.tensor_tensor(total[:, cols], ssq_win[i][:].indirect(entries(cols)), y_sq[i][:, cols], ALU.add)
             root(i, total)
 
         def product(i):
-            step[i] = arena.tile([P, S], F32, name="step%d" % i, offset=STEP_AT[i] * KB)
             for cols in pieces(i):
-                nc.gpsimd.tensor_tensor(step[i][:, cols], y_sb[i][:, cols], inv_root[i][:, cols], ALU.mult)
+                step[i, cols.start] = arena.tile(
+                    [P, cols.stop - cols.start], F32, name="step%d_%d" % (i, cols.start), offset=STEP_AT[i] * KB + 4 * cols.start
+                )
+                nc.gpsimd.tensor_tensor(step[i, cols.start][:], y_sb[i][:, cols], inv_root[i][:, cols], ALU.mult)
 
         def scatter_and_store(i):
             if i in FUSED_PAR:
                 nc.vector.tensor_copy(par_win[i][:].indirect(ent_sb[:]), par_got[i][:])
             else:
-                nc.vector.tensor_tensor(par_win[i][:].indirect(ent_sb[:]), par_got[i][:], step[i][:], ALU.add)
+                nc.vector.tensor_tensor(par_win[i][:].indirect(ent_sb[:]), par_got[i][:], step[i, 0][:], ALU.add)
             nc.sync.dma_start(out_rows[:, ROW[i], :], par_win[i][:])
 
         def round_half(i, h):
@@ -209,9 +211,9 @@ def tile_picked_adagr8_none_po_kernel(
         square(C)
         square(D)
 
-        load_ssq(D)
+        load_ssq(C)
         ssq_got = held.tile([P, S], F32, name="ssq_got")
-        nc.vector.tensor_copy(ssq_got[:], ssq_win[D][:].indirect(ent_sb[:]))
+        nc.vector.tensor_copy(ssq_got[:], ssq_win[C][:].indirect(ent_sb[:]))
         product(A)
         for i in (B, C, D):
             copy_y(i)
@@ -219,22 +221,22 @@ def tile_picked_adagr8_none_po_kernel(
         load_par(A)
         gather_par(A)
         scatter_and_store(A)
-        total_d = arena.tile([P, S], F32, name="total_d", offset=TOTAL_AT[D] * KB)
-        nc.gpsimd.tensor_tensor(total_d[:], ssq_got[:], y_sq[D][:], ALU.add)
+        total_c = arena.tile([P, S], F32, name="total_c", offset=TOTAL_AT[C] * KB)
+        nc.gpsimd.tensor_tensor(total_c[:], ssq_got[:], y_sq[C][:], ALU.add)
         product(B)
-        root(D, total_d)
-        round_half(A, 0)
+        root(C, total_c)
+        for h in range(2):
+            round_half(A, h)
 
-        load_ssq(C)
+        load_ssq(D)
         load_par(B)
         load_par(D)
         gather_par(B)
-        gather_ssq_and_root(C)
+        gather_ssq_and_root(D)
         scatter_and_store(B)
         gather_par(D)
         product(C)
         product(D)
-        round_half(A, 1)
         for h in range(2):
             round_half(B, h)
         scatter_and_store(C)

@@ -30,14 +30,14 @@ W_BF_AT = 24
 WORD_AT = 78
 SCALE_AT = 44
 CODES_AT = 43
-PAR_AT = (26, 78, 150, 40)
+PAR_AT = (26, 78, 32, 40)
 SSQ_AT = (14, 18, 22, 82)
 SQUARE_AT = (60, 72, 14, 16)
 Y_AT = (70, 63, 65, 18)
 TOTAL_AT = (64, 74, 91, 13)
 STEP_AT = (90, 14, 16, 98)
 GOT_AT = (52, 54, 56, 82)
-ROUNDED_AT = (92, 88)
+ROUNDED_AT = (92, 90, 12)
 
 
 def tile_picked_adagr8_none_po_kernel(
@@ -133,7 +133,7 @@ def tile_picked_adagr8_none_po_kernel(
         inv_root = {}
         step = {}
         rounded = {}
-        col_half = U // 2
+        parts = (slice(0, 512), slice(512, 768), slice(768, U))
 
         def pieces(i):
             return entry_halves if i in FUSED_PAR else [slice(0, S)]
@@ -196,9 +196,9 @@ def tile_picked_adagr8_none_po_kernel(
         def round_half(i, h):
             if i == A:
                 rounded[h] = arena.tile(
-                    [P, col_half, PACK], BF16, name="rounded%d" % h, align_bytes=64, offset=ROUNDED_AT[h] * KB
+                    [P, parts[h].stop - parts[h].start, PACK], BF16, name="rounded%d" % h, align_bytes=64, offset=ROUNDED_AT[h] * KB
                 )
-            nc.scalar.copy(rounded[h][:, :, ROW[i]], par_win[i][:, h * col_half : (h + 1) * col_half])
+            nc.scalar.copy(rounded[h][:, :, ROW[i]], par_win[i][:, parts[h]])
 
         load_par(C)
         gather_par(C)
@@ -233,14 +233,15 @@ def tile_picked_adagr8_none_po_kernel(
         load_par(D)
         gather_par(B)
         gather_ssq_and_root(D)
+        round_half(A, 2)
         scatter_and_store(B)
         gather_par(D)
         product(C)
         product(D)
-        for h in range(2):
+        for h in range(len(parts)):
             round_half(B, h)
         scatter_and_store(C)
-        for h in range(2):
+        for h in range(len(parts)):
             round_half(C, h)
         scatter_and_store(D)
 
@@ -248,8 +249,8 @@ def tile_picked_adagr8_none_po_kernel(
         chunks = [slice(a, b) for a, b in zip(edges, edges[1:])]
 
         def rounded_chunk(cols):
-            start = cols.start % col_half
-            return rounded[cols.start // col_half][:, start : start + cols.stop - cols.start, :]
+            h = max(n for n, part in enumerate(parts) if part.start <= cols.start)
+            return rounded[h][:, cols.start - parts[h].start : cols.stop - parts[h].start, :]
 
         for cols in chunks[2:]:
             nc.scalar.copy(rounded_chunk(cols)[:, :, ROW[D]], par_win[D][:, cols])

@@ -21,8 +21,7 @@ GROUP = 16
 QUAD = 32
 
 A, B, C, D = range(PACK)
-ROW = (2, 0, 1, 3)
-FUSED_PAR = (A, B)
+ROW = (0, 1, 2, 3)
 
 KB = 1024
 W_RAW_AT = (48, 16)
@@ -30,14 +29,16 @@ W_BF_AT = 24
 WORD_AT = 78
 SCALE_AT = 44
 CODES_AT = 43
-PAR_AT = (26, 78, 32, 40)
-SSQ_AT = (14, 18, 22, 82)
-SQUARE_AT = (60, 72, 14, 16)
-Y_AT = (70, 63, 65, 18)
-TOTAL_AT = (64, 74, 91, 13)
-STEP_AT = (90, 14, 16, 98)
-GOT_AT = (52, 54, 56, 82)
-ROUNDED_AT = (92, 90, 12)
+SSQ_AT = (14, 18, 26, 82)
+PAR_AT = (22, 32, 78, 40)
+SQUARE_AT = (60, 62, 14, 72)
+Y_AT = {B: 26, C: 61, D: 82}
+SSQ_GOT_AT = {C: 72, D: 88}
+PAR_GOT_AT = {B: 100, C: 63, D: 90}
+TOTAL_AT = {C: 62, D: 100}
+STEP_AT = {B: 72, C: 100, D: 92}
+NEW_AT = {A: 70, B: 76, C: 86}
+PAIR_AT = (100.5, 98.5, 101.5, 82)
 
 
 def tile_picked_adagr8_none_po_kernel(
@@ -125,149 +126,149 @@ def tile_picked_adagr8_none_po_kernel(
                 )
                 y_banks[i].append((cols, bank))
 
-        y_sq = {}
-        y_sb = {}
-        par_win = {}
-        par_got = {}
-        ssq_win = {}
-        inv_root = {}
-        step = {}
-        rounded = {}
-        parts = (slice(0, 512), slice(512, 768), slice(768, U))
-
-        def pieces(i):
-            return entry_halves if i in FUSED_PAR else [slice(0, S)]
+        y_sq, y_sb, par_win, par_got, ssq_win, ssq_got = {}, {}, {}, {}, {}, {}
+        total, inv_root, step, new, pair = {}, {}, {}, {}, {}
 
         def entries(cols):
             return ent_sb[:, cols.start // GROUP : cols.stop // GROUP]
 
+        def placed(name, width, at):
+            return arena.tile([P, width], F32, name=name, offset=at * KB)
+
+        def load_par(i):
+            par_win[i] = placed("par_win%d" % i, U, PAR_AT[i])
+            nc.sync.dma_start(par_win[i][:], par_rows[:, ROW[i], :])
+
+        def load_ssq(i):
+            ssq_win[i] = placed("ssq_win%d" % i, U, SSQ_AT[i])
+            nc.sync.dma_start(ssq_win[i][:], ssq_rows[:, ROW[i], :])
+
         def square(i):
-            y_sq[i] = arena.tile([P, S], F32, name="y_sq%d" % i, offset=SQUARE_AT[i] * KB)
+            y_sq[i] = placed("y_sq%d" % i, S, SQUARE_AT[i])
             for cols, bank in y_banks[i]:
                 nc.scalar.activation(y_sq[i][:, cols], bank[:], ACT.Square)
 
         def copy_y(i):
-            y_sb[i] = arena.tile([P, S], F32, name="y_sb%d" % i, offset=Y_AT[i] * KB)
-            for cols, bank in y_banks[i]:
-                nc.scalar.activation(y_sb[i][:, cols], bank[:], ACT.Copy, scale=1.0 if i in FUSED_PAR else -1.0)
+            y_sb[i] = placed("y_sb%d" % i, S, Y_AT[i])
+            nc.scalar.activation(y_sb[i][:], y_banks[i][0][1][:], ACT.Copy, scale=-1.0 if i == D else 1.0)
 
-        def load_par(i):
-            par_win[i] = arena.tile([P, U], F32, name="par_win%d" % i, offset=PAR_AT[i] * KB)
-            nc.sync.dma_start(par_win[i][:], par_rows[:, ROW[i], :])
+        def scalar_gather_ssq(i):
+            ssq_got[i] = placed("ssq_got%d" % i, S, SSQ_GOT_AT[i])
+            nc.scalar.activation(ssq_got[i][:], ssq_win[i][:].indirect(ent_sb[:]), ACT.Copy)
 
-        def load_ssq(i):
-            ssq_win[i] = arena.tile([P, U], F32, name="ssq_win%d" % i, offset=SSQ_AT[i] * KB)
-            nc.sync.dma_start(ssq_win[i][:], ssq_rows[:, ROW[i], :])
+        def scalar_gather_par(i):
+            par_got[i] = placed("par_got%d" % i, S, PAR_GOT_AT[i])
+            nc.scalar.activation(par_got[i][:], par_win[i][:].indirect(ent_sb[:]), ACT.Copy)
 
-        def gather_par(i):
-            par_got[i] = arena.tile([P, S], F32, name="par_got%d" % i, offset=GOT_AT[i] * KB)
-            if i in FUSED_PAR:
-                for cols in pieces(i):
-                    nc.vector.tensor_tensor(
-                        par_got[i][:, cols], par_win[i][:].indirect(entries(cols)), step[i, cols.start][:], ALU.subtract
-                    )
-            else:
-                nc.vector.tensor_copy(par_got[i][:], par_win[i][:].indirect(ent_sb[:]))
+        def add(i):
+            total[i] = placed("total%d" % i, S, TOTAL_AT[i])
+            nc.gpsimd.tensor_tensor(total[i][:], ssq_got[i][:], y_sq[i][:], ALU.add)
 
-        def root(i, total):
+        def root(i):
             inv_root[i] = held.tile([P, S], F32, name="inv_root%d" % i)
-            nc.scalar.activation(inv_root[i][:], total[:], ACT.Abs_reciprocal_sqrt)
-
-        def gather_ssq_and_root(i):
-            total = arena.tile([P, S], F32, name="total%d" % i, offset=TOTAL_AT[i] * KB)
-            for cols in entry_halves if i == A else [slice(0, S)]:
-                nc.vector.tensor_tensor(total[:, cols], ssq_win[i][:].indirect(entries(cols)), y_sq[i][:, cols], ALU.add)
-            root(i, total)
+            nc.scalar.activation(inv_root[i][:], total[i][:], ACT.Abs_reciprocal_sqrt)
 
         def product(i):
-            for cols in pieces(i):
-                step[i, cols.start] = arena.tile(
-                    [P, cols.stop - cols.start], F32, name="step%d_%d" % (i, cols.start), offset=STEP_AT[i] * KB + 4 * cols.start
-                )
-                nc.gpsimd.tensor_tensor(step[i, cols.start][:], y_sb[i][:, cols], inv_root[i][:, cols], ALU.mult)
+            step[i] = placed("step%d" % i, S, STEP_AT[i])
+            nc.gpsimd.tensor_tensor(step[i][:], y_sb[i][:], inv_root[i][:], ALU.mult)
+
+        def difference(i):
+            new[i] = placed("new%d" % i, S, NEW_AT[i])
+            nc.gpsimd.tensor_tensor(new[i][:], par_got[i][:], step[i][:], ALU.subtract)
 
         def scatter_and_store(i):
-            if i in FUSED_PAR:
-                nc.vector.tensor_copy(par_win[i][:].indirect(ent_sb[:]), par_got[i][:])
+            if i == D:
+                nc.vector.tensor_tensor(par_win[i][:].indirect(ent_sb[:]), par_got[i][:], step[i][:], ALU.add)
             else:
-                nc.vector.tensor_tensor(par_win[i][:].indirect(ent_sb[:]), par_got[i][:], step[i, 0][:], ALU.add)
+                nc.vector.tensor_copy(par_win[i][:].indirect(ent_sb[:]), new[i][:])
             nc.sync.dma_start(out_rows[:, ROW[i], :], par_win[i][:])
 
-        def round_half(i, h):
-            if i == A:
-                rounded[h] = arena.tile(
-                    [P, parts[h].stop - parts[h].start, PACK], BF16, name="rounded%d" % h, align_bytes=64, offset=ROUNDED_AT[h] * KB
-                )
-            nc.scalar.copy(rounded[h][:, :, ROW[i]], par_win[i][:, parts[h]])
-
-        load_par(C)
-        gather_par(C)
-        square(A)
-        square(B)
-        copy_y(A)
-        for i in (A, B):
-            load_ssq(i)
-            gather_ssq_and_root(i)
-        square(C)
-        square(D)
-
-        load_ssq(C)
-        ssq_got = held.tile([P, S], F32, name="ssq_got")
-        nc.vector.tensor_copy(ssq_got[:], ssq_win[C][:].indirect(ent_sb[:]))
-        product(A)
-        for i in (B, C, D):
-            copy_y(i)
-
-        load_par(A)
-        gather_par(A)
-        scatter_and_store(A)
-        total_c = arena.tile([P, S], F32, name="total_c", offset=TOTAL_AT[C] * KB)
-        nc.gpsimd.tensor_tensor(total_c[:], ssq_got[:], y_sq[C][:], ALU.add)
-        product(B)
-        root(C, total_c)
-        for h in range(2):
-            round_half(A, h)
-
-        load_ssq(D)
-        load_par(B)
-        load_par(D)
-        gather_par(B)
-        gather_ssq_and_root(D)
-        round_half(A, 2)
-        scatter_and_store(B)
-        gather_par(D)
-        product(C)
-        product(D)
-        for h in range(len(parts)):
-            round_half(B, h)
-        scatter_and_store(C)
-        for h in range(len(parts)):
-            round_half(C, h)
-        scatter_and_store(D)
-
-        edges = (0, 256, 512, 768, 896, 1024)
+        edges = (0, 128, 384, 768, 1024)
         chunks = [slice(a, b) for a, b in zip(edges, edges[1:])]
 
-        def rounded_chunk(cols):
-            h = max(n for n, part in enumerate(parts) if part.start <= cols.start)
-            return rounded[h][:, cols.start - parts[h].start : cols.stop - parts[h].start, :]
+        def round_into_pair(i, c):
+            cols = chunks[c]
+            if i == A:
+                pair[c] = arena.tile(
+                    [P, 2, cols.stop - cols.start, 2], BF16, name="pair%d" % c, offset=int(PAIR_AT[c] * KB)
+                )
+            nc.scalar.copy(pair[c][:, i // 2, :, i % 2], par_win[i][:, cols])
 
-        for cols in chunks[2:]:
-            nc.scalar.copy(rounded_chunk(cols)[:, :, ROW[D]], par_win[D][:, cols])
-        for cols in chunks[:2]:
-            nc.vector.tensor_copy(rounded_chunk(cols)[:, :, ROW[D]], par_win[D][:, cols])
+        half = S // 2
+        first, second = entry_halves
+        for load, i in ((load_par, B), (load_ssq, A), (load_ssq, B), (load_par, A), (load_ssq, C), (load_par, C), (load_ssq, D), (load_par, D)):
+            load(i)
+
+        par_got[B] = placed("par_got_b", S, PAR_GOT_AT[B])
+        nc.vector.tensor_copy(par_got[B][:], par_win[B][:].indirect(ent_sb[:]))
+        square(A)
+        square(B)
+        total_a = placed("total_a", S, 64)
+        inv_root[A] = held.tile([P, S], F32, name="inv_root_a")
+        for cols in entry_halves:
+            nc.vector.tensor_tensor(total_a[:, cols], ssq_win[A][:].indirect(entries(cols)), y_sq[A][:, cols], ALU.add)
+        for cols in entry_halves:
+            nc.scalar.activation(inv_root[A][:, cols], total_a[:, cols], ACT.Abs_reciprocal_sqrt)
+        total_b0 = placed("total_b0", half, 66)
+        nc.vector.tensor_tensor(total_b0[:], ssq_win[B][:].indirect(entries(first)), y_sq[B][:, first], ALU.add)
+        square(C)
+        step_a = [placed("step_a%d" % h, half, 68 + h) for h in range(2)]
+        for h, (cols, bank) in enumerate(y_banks[A]):
+            nc.vector.tensor_tensor(step_a[h][:], bank[:], inv_root[A][:, cols], ALU.mult)
+        new[A] = placed("new_a", S, NEW_AT[A])
+        for h, cols in enumerate(entry_halves):
+            nc.vector.tensor_tensor(new[A][:, cols], par_win[A][:].indirect(entries(cols)), step_a[h][:], ALU.subtract)
+        total_b1 = placed("total_b1", half, 68)
+        nc.vector.tensor_tensor(total_b1[:], ssq_win[B][:].indirect(entries(second)), y_sq[B][:, second], ALU.add)
+        scatter_and_store(A)
+
+        scalar_gather_ssq(C)
+        inv_root[B] = placed("inv_root_b", S, 28)
+        nc.scalar.activation(inv_root[B][:, first], total_b0[:], ACT.Abs_reciprocal_sqrt)
+        copy_y(B)
+        nc.scalar.activation(inv_root[B][:, second], total_b1[:], ACT.Abs_reciprocal_sqrt)
+        add(C)
+        product(B)
+        root(C)
+        copy_y(C)
+        difference(B)
+        scatter_and_store(B)
+        scalar_gather_par(C)
+        square(D)
+        product(C)
+        scalar_gather_ssq(D)
+        difference(C)
+        scatter_and_store(C)
+        copy_y(D)
+        add(D)
+        scalar_gather_par(D)
+        root(D)
+        product(D)
+        scatter_and_store(D)
+        for i in (A, B, C, D):
+            for c in range(len(chunks)):
+                round_into_pair(i, c)
 
         out_codes = held.tile([P, U], U32, name="out_codes", align_bytes=64)
         out_scale = held.tile([P, U], U8, name="out_scale", align_bytes=64)
         words_hbm = out_1[0].rearrange("p n t -> p (n t)").bitcast(I32)
+        rounded = []
+        for c, cols in enumerate(chunks):
+            tile_c = held.tile([P, cols.stop - cols.start, PACK], BF16, name="rounded%d" % c, align_bytes=64)
+            rounded.append(tile_c)
+            words = pair[c][:].rearrange("p h u e -> p h (u e)")
+            if c == len(chunks) - 1:
+                nc.scalar.copy(tile_c[:].bitcast(U32), words.bitcast(U32).rearrange("p h u -> p u h"))
+            else:
+                nc.vector.tensor_copy(tile_c[:].bitcast(I32), words.bitcast(I32).rearrange("p h u -> p u h"))
         stored = 0
         for c, cols in enumerate(chunks):
             nc.vector.quantize_mx(
                 out=out_codes[:, cols].bitcast(FP8X4),
                 scales=out_scale[:, cols],
-                in_=rounded_chunk(cols).rearrange("p u t -> p (u t)"),
+                in_=rounded[c][:].rearrange("p u t -> p (u t)"),
             )
-            if c not in (0, 2):
+            if c != 0:
                 nc.sync.dma_start(words_hbm[:, stored : cols.stop], out_codes[:, stored : cols.stop].bitcast(I32))
                 stored = cols.stop
         for q in range(P // QUAD):

@@ -21,7 +21,7 @@ GROUP = 16
 QUAD = 32
 
 A, B, C, D = range(PACK)
-ROW = (0, 1, 2, 3)
+ROW = (0, 2, 3, 1)
 
 KB = 1024
 W_RAW_AT = (48, 16)
@@ -31,14 +31,14 @@ SCALE_AT = 44
 CODES_AT = 43
 SSQ_AT = (14, 18, 26, 82)
 PAR_AT = (22, 32, 78, 40)
-SQUARE_AT = (60, 62, 14, 72)
-Y_AT = {B: 26, C: 61, D: 82}
-SSQ_GOT_AT = {C: 72, D: 88}
-PAR_GOT_AT = {B: 100, C: 63, D: 90}
-TOTAL_AT = {C: 62, D: 100}
-STEP_AT = {B: 72, C: 100, D: 92}
-NEW_AT = {A: 70, B: 76, C: 86}
-PAIR_AT = (100.5, 98.5, 101.5, 82)
+SQUARE_AT = (60, 62, 14, 110)
+Y_AT = {B: 64, D: 82}
+SSQ_GOT_AT = {D: 88}
+PAR_GOT_AT = {B: 100, C: 68, D: 22}
+TOTAL_AT = {D: 100}
+STEP_AT = {B: 14, C: 72, D: 68}
+NEW_AT = {A: 70, B: 76, C: 88}
+PAIR_AT = (97.25, 100.25, 101.5, 82)
 
 
 def tile_picked_adagr8_none_po_kernel(
@@ -160,14 +160,6 @@ def tile_picked_adagr8_none_po_kernel(
             par_got[i] = placed("par_got%d" % i, S, PAR_GOT_AT[i])
             nc.scalar.activation(par_got[i][:], par_win[i][:].indirect(ent_sb[:]), ACT.Copy)
 
-        def add(i):
-            total[i] = placed("total%d" % i, S, TOTAL_AT[i])
-            nc.gpsimd.tensor_tensor(total[i][:], ssq_got[i][:], y_sq[i][:], ALU.add)
-
-        def root(i):
-            inv_root[i] = held.tile([P, S], F32, name="inv_root%d" % i)
-            nc.scalar.activation(inv_root[i][:], total[i][:], ACT.Abs_reciprocal_sqrt)
-
         def product(i):
             step[i] = placed("step%d" % i, S, STEP_AT[i])
             nc.gpsimd.tensor_tensor(step[i][:], y_sb[i][:], inv_root[i][:], ALU.mult)
@@ -183,94 +175,110 @@ def tile_picked_adagr8_none_po_kernel(
                 nc.vector.tensor_copy(par_win[i][:].indirect(ent_sb[:]), new[i][:])
             nc.sync.dma_start(out_rows[:, ROW[i], :], par_win[i][:])
 
-        edges = (0, 128, 384, 768, 1024)
+        edges = (0, 384, 512, 896, 1024)
         chunks = [slice(a, b) for a, b in zip(edges, edges[1:])]
 
-        def round_into_pair(i, c):
+        def round_into_pair(i, c, copy=nc.scalar.copy):
             cols = chunks[c]
             if i == A:
                 pair[c] = arena.tile(
                     [P, 2, cols.stop - cols.start, 2], BF16, name="pair%d" % c, offset=int(PAIR_AT[c] * KB)
                 )
-            nc.scalar.copy(pair[c][:, i // 2, :, i % 2], par_win[i][:, cols])
+            copy(pair[c][:, ROW[i] // 2, :, ROW[i] % 2], par_win[i][:, cols])
 
         half = S // 2
         first, second = entry_halves
-        for load, i in ((load_par, B), (load_ssq, A), (load_ssq, B), (load_par, A), (load_ssq, C), (load_par, C), (load_ssq, D), (load_par, D)):
+        for load, i in ((load_par, B), (load_ssq, A), (load_ssq, B), (load_ssq, C), (load_par, A), (load_ssq, D), (load_par, C), (load_par, D)):
             load(i)
 
         par_got[B] = placed("par_got_b", S, PAR_GOT_AT[B])
         nc.vector.tensor_copy(par_got[B][:], par_win[B][:].indirect(ent_sb[:]))
+        def fused_total(i, out, cols):
+            nc.vector.tensor_tensor(out, ssq_win[i][:].indirect(entries(cols)), y_sq[i][:, cols], ALU.add)
+
+        def root_of(i, cols, source):
+            nc.scalar.activation(inv_root[i][:, cols], source, ACT.Abs_reciprocal_sqrt)
+
+        for i in (A, B, C, D):
+            inv_root[i] = held.tile([P, S], F32, name="inv_root%d" % i)
         square(A)
         square(B)
-        total_a = placed("total_a", S, 64)
-        inv_root[A] = held.tile([P, S], F32, name="inv_root_a")
+        total[A] = placed("total_a", S, 64)
         for cols in entry_halves:
-            nc.vector.tensor_tensor(total_a[:, cols], ssq_win[A][:].indirect(entries(cols)), y_sq[A][:, cols], ALU.add)
+            fused_total(A, total[A][:, cols], cols)
         for cols in entry_halves:
-            nc.scalar.activation(inv_root[A][:, cols], total_a[:, cols], ACT.Abs_reciprocal_sqrt)
-        total_b0 = placed("total_b0", half, 66)
-        nc.vector.tensor_tensor(total_b0[:], ssq_win[B][:].indirect(entries(first)), y_sq[B][:, first], ALU.add)
+            root_of(A, cols, total[A][:, cols])
+        total[B] = placed("total_b", S, 66)
+        fused_total(B, total[B][:], slice(0, S))
         square(C)
+        root_of(B, slice(0, S), total[B][:])
         step_a = [placed("step_a%d" % h, half, 68 + h) for h in range(2)]
         for h, (cols, bank) in enumerate(y_banks[A]):
             nc.vector.tensor_tensor(step_a[h][:], bank[:], inv_root[A][:, cols], ALU.mult)
+        total_c0 = placed("total_c0", half, 110)
+        fused_total(C, total_c0[:], first)
         new[A] = placed("new_a", S, NEW_AT[A])
         for h, cols in enumerate(entry_halves):
             nc.vector.tensor_tensor(new[A][:, cols], par_win[A][:].indirect(entries(cols)), step_a[h][:], ALU.subtract)
-        total_b1 = placed("total_b1", half, 68)
-        nc.vector.tensor_tensor(total_b1[:], ssq_win[B][:].indirect(entries(second)), y_sq[B][:, second], ALU.add)
+        total_c1 = placed("total_c1", half, 68)
+        fused_total(C, total_c1[:], second)
         scatter_and_store(A)
 
-        scalar_gather_ssq(C)
-        inv_root[B] = placed("inv_root_b", S, 28)
-        nc.scalar.activation(inv_root[B][:, first], total_b0[:], ACT.Abs_reciprocal_sqrt)
         copy_y(B)
-        nc.scalar.activation(inv_root[B][:, second], total_b1[:], ACT.Abs_reciprocal_sqrt)
-        add(C)
+        root_of(C, first, total_c0[:])
         product(B)
-        root(C)
-        copy_y(C)
+        root_of(C, second, total_c1[:])
+        step[C] = placed("step_c", S, STEP_AT[C])
+        nc.vector.tensor_tensor(step[C][:], y_banks[C][0][1][:], inv_root[C][:], ALU.mult)
+        square(D)
+        scalar_gather_ssq(D)
         difference(B)
         scatter_and_store(B)
         scalar_gather_par(C)
-        square(D)
-        product(C)
-        scalar_gather_ssq(D)
+        total[D] = placed("total_d", S, TOTAL_AT[D])
+        nc.gpsimd.tensor_tensor(total[D][:], ssq_got[D][:], y_sq[D][:], ALU.add)
+        copy_y(D)
+        root_of(D, slice(0, S), total[D][:])
         difference(C)
         scatter_and_store(C)
-        copy_y(D)
-        add(D)
-        scalar_gather_par(D)
-        root(D)
         product(D)
+        for c in range(len(chunks)):
+            round_into_pair(A, c)
+        scalar_gather_par(D)
         scatter_and_store(D)
-        for i in (A, B, C, D):
+        for i in (B, C):
             for c in range(len(chunks)):
                 round_into_pair(i, c)
+        round_into_pair(D, 0, nc.vector.tensor_copy)
 
         out_codes = held.tile([P, U], U32, name="out_codes", align_bytes=64)
         out_scale = held.tile([P, U], U8, name="out_scale", align_bytes=64)
         words_hbm = out_1[0].rearrange("p n t -> p (n t)").bitcast(I32)
-        rounded = []
-        for c, cols in enumerate(chunks):
-            tile_c = held.tile([P, cols.stop - cols.start, PACK], BF16, name="rounded%d" % c, align_bytes=64)
-            rounded.append(tile_c)
-            words = pair[c][:].rearrange("p h u e -> p h (u e)")
-            if c == len(chunks) - 1:
-                nc.scalar.copy(tile_c[:].bitcast(U32), words.bitcast(U32).rearrange("p h u -> p u h"))
-            else:
-                nc.vector.tensor_copy(tile_c[:].bitcast(I32), words.bitcast(I32).rearrange("p h u -> p u h"))
-        stored = 0
-        for c, cols in enumerate(chunks):
+        parts = (slice(0, 512), chunks[2], chunks[3])
+        rounded = [
+            held.tile([P, part.stop - part.start, PACK], BF16, name="rounded%d" % n, align_bytes=64)
+            for n, part in enumerate(parts)
+        ]
+
+        def merge(c, copy, word):
+            n = max(0, c - 1)
+            cols = slice(chunks[c].start - parts[n].start, chunks[c].stop - parts[n].start)
+            words = pair[c][:].rearrange("p h u e -> p h (u e)").bitcast(word)
+            copy(rounded[n][:, cols, :].bitcast(word), words.rearrange("p h u -> p u h"))
+
+        round_into_pair(D, 1)
+        merge(1, nc.vector.tensor_copy, I32)
+        merge(0, nc.vector.tensor_copy, I32)
+        for c in (2, 3):
+            round_into_pair(D, c)
+            merge(c, nc.scalar.copy, U32)
+        for n, cols in enumerate(parts):
             nc.vector.quantize_mx(
                 out=out_codes[:, cols].bitcast(FP8X4),
                 scales=out_scale[:, cols],
-                in_=rounded[c][:].rearrange("p u t -> p (u t)"),
+                in_=rounded[n][:].rearrange("p u t -> p (u t)"),
             )
-            if c != 0:
-                nc.sync.dma_start(words_hbm[:, stored : cols.stop], out_codes[:, stored : cols.stop].bitcast(I32))
-                stored = cols.stop
+            nc.sync.dma_start(words_hbm[:, cols], out_codes[:, cols].bitcast(I32))
         for q in range(P // QUAD):
             queue = nc.scalar if q % 2 == 0 else nc.sync
             queue.dma_start(

@@ -34,11 +34,11 @@ PAR_AT = (22, 32, 78, 40)
 SQUARE_AT = (60, 62, 14, 110)
 Y_AT = {B: 64, D: 82}
 SSQ_GOT_AT = {D: 88}
-PAR_GOT_AT = {B: 100, C: 68, D: 22}
+PAR_GOT_AT = {B: 100, C: 68, D: 90}
 TOTAL_AT = {D: 100}
 STEP_AT = {B: 14, C: 72, D: 68}
 NEW_AT = {A: 70, B: 76, C: 88}
-PAIR_AT = (97.25, 100.25, 101.5, 82)
+ROUNDED_AT = (10.5, 15.5)
 
 
 def tile_picked_adagr8_none_po_kernel(
@@ -127,7 +127,7 @@ def tile_picked_adagr8_none_po_kernel(
                 y_banks[i].append((cols, bank))
 
         y_sq, y_sb, par_win, par_got, ssq_win, ssq_got = {}, {}, {}, {}, {}, {}
-        total, inv_root, step, new, pair = {}, {}, {}, {}, {}
+        total, inv_root, step, new, rounded = {}, {}, {}, {}, {}
 
         def entries(cols):
             return ent_sb[:, cols.start // GROUP : cols.stop // GROUP]
@@ -175,16 +175,14 @@ def tile_picked_adagr8_none_po_kernel(
                 nc.vector.tensor_copy(par_win[i][:].indirect(ent_sb[:]), new[i][:])
             nc.sync.dma_start(out_rows[:, ROW[i], :], par_win[i][:])
 
-        edges = (0, 384, 512, 896, 1024)
-        chunks = [slice(a, b) for a, b in zip(edges, edges[1:])]
+        parts = (slice(0, U // 2), slice(U // 2, U))
 
-        def round_into_pair(i, c, copy=nc.scalar.copy):
-            cols = chunks[c]
+        def round_part(i, h, copy=nc.scalar.copy):
             if i == A:
-                pair[c] = arena.tile(
-                    [P, 2, cols.stop - cols.start, 2], BF16, name="pair%d" % c, offset=int(PAIR_AT[c] * KB)
+                rounded[h] = arena.tile(
+                    [P, U // 2, PACK], BF16, name="rounded%d" % h, align_bytes=64, offset=int(ROUNDED_AT[h] * KB)
                 )
-            copy(pair[c][:, ROW[i] // 2, :, ROW[i] % 2], par_win[i][:, cols])
+            copy(rounded[h][:, :, ROW[i]], par_win[i][:, parts[h]])
 
         half = S // 2
         first, second = entry_halves
@@ -238,47 +236,43 @@ def tile_picked_adagr8_none_po_kernel(
         total[D] = placed("total_d", S, TOTAL_AT[D])
         nc.gpsimd.tensor_tensor(total[D][:], ssq_got[D][:], y_sq[D][:], ALU.add)
         copy_y(D)
+        scalar_gather_par(D)
+        round_part(A, 0)
         root_of(D, slice(0, S), total[D][:])
         difference(C)
         scatter_and_store(C)
+        round_part(A, 1, nc.gpsimd.tensor_copy)
         product(D)
-        for c in range(len(chunks)):
-            round_into_pair(A, c)
-        scalar_gather_par(D)
         scatter_and_store(D)
         for i in (B, C):
-            for c in range(len(chunks)):
-                round_into_pair(i, c)
-        round_into_pair(D, 0, nc.vector.tensor_copy)
+            for h in range(2):
+                round_part(i, h)
+
+        edges = (0, 256, 512, 768, 896, 1024)
+        chunks = [slice(a, b) for a, b in zip(edges, edges[1:])]
+
+        def rounded_chunk(cols):
+            h = max(n for n, part in enumerate(parts) if part.start <= cols.start)
+            return rounded[h][:, cols.start - parts[h].start : cols.stop - parts[h].start, :]
+
+        for cols in chunks[2:]:
+            nc.scalar.copy(rounded_chunk(cols)[:, :, ROW[D]], par_win[D][:, cols])
+        for cols in chunks[:2]:
+            nc.vector.tensor_copy(rounded_chunk(cols)[:, :, ROW[D]], par_win[D][:, cols])
 
         out_codes = held.tile([P, U], U32, name="out_codes", align_bytes=64)
         out_scale = held.tile([P, U], U8, name="out_scale", align_bytes=64)
         words_hbm = out_1[0].rearrange("p n t -> p (n t)").bitcast(I32)
-        parts = (slice(0, 512), chunks[2], chunks[3])
-        rounded = [
-            held.tile([P, part.stop - part.start, PACK], BF16, name="rounded%d" % n, align_bytes=64)
-            for n, part in enumerate(parts)
-        ]
-
-        def merge(c, copy, word):
-            n = max(0, c - 1)
-            cols = slice(chunks[c].start - parts[n].start, chunks[c].stop - parts[n].start)
-            words = pair[c][:].rearrange("p h u e -> p h (u e)").bitcast(word)
-            copy(rounded[n][:, cols, :].bitcast(word), words.rearrange("p h u -> p u h"))
-
-        round_into_pair(D, 1)
-        merge(1, nc.vector.tensor_copy, I32)
-        merge(0, nc.vector.tensor_copy, I32)
-        for c in (2, 3):
-            round_into_pair(D, c)
-            merge(c, nc.scalar.copy, U32)
-        for n, cols in enumerate(parts):
+        stored = 0
+        for c, cols in enumerate(chunks):
             nc.vector.quantize_mx(
                 out=out_codes[:, cols].bitcast(FP8X4),
                 scales=out_scale[:, cols],
-                in_=rounded[n][:].rearrange("p u t -> p (u t)"),
+                in_=rounded_chunk(cols).rearrange("p u t -> p (u t)"),
             )
-            nc.sync.dma_start(words_hbm[:, cols], out_codes[:, cols].bitcast(I32))
+            if c not in (0, 2):
+                nc.sync.dma_start(words_hbm[:, stored : cols.stop], out_codes[:, stored : cols.stop].bitcast(I32))
+                stored = cols.stop
         for q in range(P // QUAD):
             queue = nc.scalar if q % 2 == 0 else nc.sync
             queue.dma_start(

@@ -21,7 +21,7 @@ GROUP = 16
 QUAD = 32
 
 A, B, C, D = range(PACK)
-ROW = (0, 2, 3, 1)
+ROW = (0, 2, 1, 3)
 
 KB = 1024
 W_RAW_AT = (48, 16)
@@ -36,9 +36,10 @@ Y_AT = {B: 64, D: 82}
 SSQ_GOT_AT = {D: 88}
 PAR_GOT_AT = {B: 100, C: 68, D: 90}
 TOTAL_AT = {D: 100}
-STEP_AT = {B: 14, C: 72, D: 68}
+STEP_AT = {B: 14, C: 72, D: 92}
 NEW_AT = {A: 70, B: 76, C: 88}
-ROUNDED_AT = (10.5, 15.5)
+ROOT_D_AT = 120
+ROUNDED_AT = (116.5, 15.5)
 
 
 def tile_picked_adagr8_none_po_kernel(
@@ -133,7 +134,7 @@ def tile_picked_adagr8_none_po_kernel(
             return ent_sb[:, cols.start // GROUP : cols.stop // GROUP]
 
         def placed(name, width, at):
-            return arena.tile([P, width], F32, name=name, offset=at * KB)
+            return arena.tile([P, width], F32, name=name, offset=int(at * KB))
 
         def load_par(i):
             par_win[i] = placed("par_win%d" % i, U, PAR_AT[i])
@@ -178,7 +179,7 @@ def tile_picked_adagr8_none_po_kernel(
         parts = (slice(0, U // 2), slice(U // 2, U))
 
         def round_part(i, h, copy=nc.scalar.copy):
-            if i == A:
+            if h not in rounded:
                 rounded[h] = arena.tile(
                     [P, U // 2, PACK], BF16, name="rounded%d" % h, align_bytes=64, offset=int(ROUNDED_AT[h] * KB)
                 )
@@ -197,7 +198,7 @@ def tile_picked_adagr8_none_po_kernel(
         def root_of(i, cols, source):
             nc.scalar.activation(inv_root[i][:, cols], source, ACT.Abs_reciprocal_sqrt)
 
-        for i in (A, B, C, D):
+        for i in (A, B, C):
             inv_root[i] = held.tile([P, S], F32, name="inv_root%d" % i)
         square(A)
         square(B)
@@ -237,16 +238,21 @@ def tile_picked_adagr8_none_po_kernel(
         nc.gpsimd.tensor_tensor(total[D][:], ssq_got[D][:], y_sq[D][:], ALU.add)
         copy_y(D)
         scalar_gather_par(D)
-        round_part(A, 0)
-        root_of(D, slice(0, S), total[D][:])
+        round_part(A, 1)
+        root_d = [placed("inv_root_d%d" % h, half, ROOT_D_AT + h) for h in range(2)]
+        for h, cols in enumerate(entry_halves):
+            nc.scalar.activation(root_d[h][:], total[D][:, cols], ACT.Abs_reciprocal_sqrt)
         difference(C)
         scatter_and_store(C)
-        round_part(A, 1, nc.gpsimd.tensor_copy)
-        product(D)
+        step[D] = placed("step_d", S, STEP_AT[D])
+        nc.gpsimd.tensor_tensor(step[D][:, first], y_sb[D][:, first], root_d[0][:], ALU.mult)
+        round_part(B, 0, nc.gpsimd.tensor_copy)
+        round_part(A, 0)
+        nc.gpsimd.tensor_tensor(step[D][:, second], y_sb[D][:, second], root_d[1][:], ALU.mult)
         scatter_and_store(D)
-        for i in (B, C):
-            for h in range(2):
-                round_part(i, h)
+        round_part(B, 1)
+        for h in range(2):
+            round_part(C, h)
 
         edges = (0, 256, 512, 768, 896, 1024)
         chunks = [slice(a, b) for a, b in zip(edges, edges[1:])]

@@ -90,11 +90,17 @@ def tile_picked_adagr8_none_po_kernel(
             )
 
         w_bf = arena.tile([P, PACK, P, PACK], BF16, name="w_bf", align_bytes=64, offset=W_BF_AT * KB)
-        m_half = w_half // PACK
-        for h, copy in enumerate((nc.scalar.copy, nc.vector.tensor_copy)):
+        w_quarter = N // 4
+        shares = (
+            (nc.scalar.copy, 0, w_raw[0][:]),
+            (nc.vector.tensor_copy, w_half, w_raw[1][:, :, :w_quarter]),
+            (nc.gpsimd.tensor_copy, w_half + w_quarter, w_raw[1][:, :, w_quarter:]),
+        )
+        for copy, start, source in shares:
+            m_cols = slice(start // PACK, (start + source.shape[2]) // PACK)
             copy(
-                w_bf[:, :, h * m_half : (h + 1) * m_half, :].rearrange("p t m j -> p m t j"),
-                w_raw[h][:].rearrange("p j (m t) -> p m t j", t=PACK),
+                w_bf[:, :, m_cols, :].rearrange("p t m j -> p m t j"),
+                source.rearrange("p j (m t) -> p m t j", t=PACK),
             )
         w_codes = held.tile([P, N], U32, name="w_codes", align_bytes=64)
         w_scale = held.tile([P, N], U8, name="w_scale", align_bytes=64)

@@ -21,7 +21,7 @@ GROUP = 16
 QUAD = 32
 
 A, B, C, D = range(PACK)
-ROW = (0, 2, 1, 3)
+ROW = (0, 2, 3, 1)
 
 KB = 1024
 W_RAW_AT = (48, 16)
@@ -30,16 +30,14 @@ WORD_AT = 78
 SCALE_AT = 44
 CODES_AT = 43
 SSQ_AT = (14, 18, 26, 82)
-PAR_AT = (22, 32, 78, 40)
-SQUARE_AT = (60, 62, 14, 110)
-Y_AT = {B: 64, D: 82}
-SSQ_GOT_AT = {D: 88}
-PAR_GOT_AT = {B: 100, C: 68, D: 90}
-TOTAL_AT = {D: 100}
-STEP_AT = {B: 14, C: 72, D: 92}
-NEW_AT = {A: 70, B: 76, C: 88}
-ROOT_D_AT = 120
-ROUNDED_AT = (116.5, 15.5)
+PAR_AT = (32, 22, 78, 40)
+SQUARE_B_AT = 60
+STEP_A_AT = (60, 64)
+TOTAL_C_AT = 64
+TOTAL_D_AT = 100
+STEP_D_AT = 104
+SSQ_GOT_D_AT = 96
+ROUNDED_AT = (94, 104)
 
 
 def tile_picked_adagr8_none_po_kernel(
@@ -133,14 +131,18 @@ def tile_picked_adagr8_none_po_kernel(
                 )
                 y_banks[i].append((cols, bank))
 
-        y_sq, y_sb, par_win, par_got, ssq_win, ssq_got = {}, {}, {}, {}, {}, {}
-        total, inv_root, step, new, rounded = {}, {}, {}, {}, {}
+        par_win, ssq_win, y_sq, total, inv_root = {}, {}, {}, {}, {}
+        par_got, ssq_got, step, new, rounded = {}, {}, {}, {}, {}
+        whole = slice(0, S)
 
         def entries(cols):
             return ent_sb[:, cols.start // GROUP : cols.stop // GROUP]
 
         def placed(name, width, at):
             return arena.tile([P, width], F32, name=name, offset=int(at * KB))
+
+        def own(name, width=S):
+            return held.tile([P, width], F32, name=name)
 
         def load_par(i):
             par_win[i] = placed("par_win%d" % i, U, PAR_AT[i])
@@ -150,36 +152,34 @@ def tile_picked_adagr8_none_po_kernel(
             ssq_win[i] = placed("ssq_win%d" % i, U, SSQ_AT[i])
             nc.sync.dma_start(ssq_win[i][:], ssq_rows[:, ROW[i], :])
 
-        def square(i):
-            y_sq[i] = placed("y_sq%d" % i, S, SQUARE_AT[i])
-            for cols, bank in y_banks[i]:
-                nc.scalar.activation(y_sq[i][:, cols], bank[:], ACT.Square)
+        for load, i in (
+            (load_par, A), (load_ssq, A), (load_ssq, B), (load_ssq, C),
+            (load_par, B), (load_ssq, D), (load_par, C), (load_par, D),
+        ):
+            load(i)
 
-        def copy_y(i):
-            y_sb[i] = placed("y_sb%d" % i, S, Y_AT[i])
-            nc.scalar.activation(y_sb[i][:], y_banks[i][0][1][:], ACT.Copy, scale=-1.0 if i == D else 1.0)
+        def scalar_gather(window, name, at=None):
+            got = own(name) if at is None else placed(name, S, at)
+            nc.scalar.activation(got[:], window[:].indirect(ent_sb[:]), ACT.Copy)
+            return got
 
-        def scalar_gather_ssq(i):
-            ssq_got[i] = placed("ssq_got%d" % i, S, SSQ_GOT_AT[i])
-            nc.scalar.activation(ssq_got[i][:], ssq_win[i][:].indirect(ent_sb[:]), ACT.Copy)
-
-        def scalar_gather_par(i):
-            par_got[i] = placed("par_got%d" % i, S, PAR_GOT_AT[i])
-            nc.scalar.activation(par_got[i][:], par_win[i][:].indirect(ent_sb[:]), ACT.Copy)
+        def root(i, cols=whole):
+            nc.scalar.activation(inv_root[i][:, cols], total[i][:, cols], ACT.Abs_reciprocal_sqrt)
 
         def product(i):
-            step[i] = placed("step%d" % i, S, STEP_AT[i])
-            nc.gpsimd.tensor_tensor(step[i][:], y_sb[i][:], inv_root[i][:], ALU.mult)
+            step[i] = placed("step_d", S, STEP_D_AT) if i == D else own("step%d" % i)
+            nc.vector.tensor_tensor(step[i][:], y_banks[i][0][1][:], inv_root[i][:], ALU.mult)
+
+        def add(i, at):
+            total[i] = placed("total%d" % i, S, at)
+            nc.gpsimd.tensor_tensor(total[i][:], ssq_got[i][:], y_sq[i][:], ALU.add)
 
         def difference(i):
-            new[i] = placed("new%d" % i, S, NEW_AT[i])
+            new[i] = own("new%d" % i)
             nc.gpsimd.tensor_tensor(new[i][:], par_got[i][:], step[i][:], ALU.subtract)
 
         def scatter_and_store(i):
-            if i == D:
-                nc.vector.tensor_tensor(par_win[i][:].indirect(ent_sb[:]), par_got[i][:], step[i][:], ALU.add)
-            else:
-                nc.vector.tensor_copy(par_win[i][:].indirect(ent_sb[:]), new[i][:])
+            nc.vector.tensor_copy(par_win[i][:].indirect(ent_sb[:]), new[i][:])
             nc.sync.dma_start(out_rows[:, ROW[i], :], par_win[i][:])
 
         parts = (slice(0, U // 2), slice(U // 2, U))
@@ -187,78 +187,69 @@ def tile_picked_adagr8_none_po_kernel(
         def round_part(i, h, copy=nc.scalar.copy):
             if h not in rounded:
                 rounded[h] = arena.tile(
-                    [P, U // 2, PACK], BF16, name="rounded%d" % h, align_bytes=64, offset=int(ROUNDED_AT[h] * KB)
+                    [P, U // 2, PACK], BF16, name="rounded%d" % h, align_bytes=64, offset=ROUNDED_AT[h] * KB
                 )
             copy(rounded[h][:, :, ROW[i]], par_win[i][:, parts[h]])
 
         half = S // 2
-        first, second = entry_halves
-        for load, i in ((load_par, B), (load_ssq, A), (load_ssq, B), (load_ssq, C), (load_par, A), (load_ssq, D), (load_par, C), (load_par, D)):
-            load(i)
+        par_got[A] = own("par_got_a")
+        nc.vector.tensor_copy(par_got[A][:], par_win[A][:].indirect(ent_sb[:]))
 
-        par_got[B] = placed("par_got_b", S, PAR_GOT_AT[B])
-        nc.vector.tensor_copy(par_got[B][:], par_win[B][:].indirect(ent_sb[:]))
-        def fused_total(i, out, cols):
-            nc.vector.tensor_tensor(out, ssq_win[i][:].indirect(entries(cols)), y_sq[i][:, cols], ALU.add)
-
-        def root_of(i, cols, source):
-            nc.scalar.activation(inv_root[i][:, cols], source, ACT.Abs_reciprocal_sqrt)
-
-        for i in (A, B, C):
-            inv_root[i] = held.tile([P, S], F32, name="inv_root%d" % i)
-        square(A)
-        square(B)
-        total[A] = placed("total_a", S, 64)
+        for i in (A, B, C, D):
+            inv_root[i] = own("inv_root%d" % i)
+        y_sq[A] = own("y_sq_a")
+        for cols, bank in y_banks[A]:
+            nc.scalar.activation(y_sq[A][:, cols], bank[:], ACT.Square)
+        y_sq_b = [placed("y_sq_b%d" % h, half, SQUARE_B_AT + h) for h in range(2)]
+        for h, cols in enumerate(entry_halves):
+            nc.scalar.activation(y_sq_b[h][:], y_banks[B][0][1][:, cols], ACT.Square)
+        total[A] = own("total_a")
         for cols in entry_halves:
-            fused_total(A, total[A][:, cols], cols)
+            nc.vector.tensor_tensor(total[A][:, cols], ssq_win[A][:].indirect(entries(cols)), y_sq[A][:, cols], ALU.add)
+        total[B] = own("total_b")
+        for h, cols in enumerate(entry_halves):
+            nc.vector.tensor_tensor(total[B][:, cols], ssq_win[B][:].indirect(entries(cols)), y_sq_b[h][:], ALU.add)
         for cols in entry_halves:
-            root_of(A, cols, total[A][:, cols])
-        total[B] = placed("total_b", S, 66)
-        fused_total(B, total[B][:], slice(0, S))
-        square(C)
-        root_of(B, slice(0, S), total[B][:])
-        step_a = [placed("step_a%d" % h, half, 68 + h) for h in range(2)]
+            root(A, cols)
+        root(B)
+        for i in (C, D):
+            y_sq[i] = own("y_sq%d" % i)
+            nc.scalar.activation(y_sq[i][:], y_banks[i][0][1][:], ACT.Square)
+
+        step_a = [placed("step_a%d" % h, half, STEP_A_AT[h]) for h in range(2)]
         for h, (cols, bank) in enumerate(y_banks[A]):
             nc.vector.tensor_tensor(step_a[h][:], bank[:], inv_root[A][:, cols], ALU.mult)
-        total_c0 = placed("total_c0", half, 110)
-        fused_total(C, total_c0[:], first)
-        new[A] = placed("new_a", S, NEW_AT[A])
+        new[A] = own("new_a")
         for h, cols in enumerate(entry_halves):
-            nc.vector.tensor_tensor(new[A][:, cols], par_win[A][:].indirect(entries(cols)), step_a[h][:], ALU.subtract)
-        total_c1 = placed("total_c1", half, 68)
-        fused_total(C, total_c1[:], second)
+            nc.vector.tensor_tensor(new[A][:, cols], par_got[A][:, cols], step_a[h][:], ALU.subtract)
+        product(B)
         scatter_and_store(A)
 
-        copy_y(B)
-        root_of(C, first, total_c0[:])
-        product(B)
-        root_of(C, second, total_c1[:])
-        step[C] = placed("step_c", S, STEP_AT[C])
-        nc.vector.tensor_tensor(step[C][:], y_banks[C][0][1][:], inv_root[C][:], ALU.mult)
-        square(D)
-        scalar_gather_ssq(D)
+        ssq_got[C] = scalar_gather(ssq_win[C], "ssq_got_c")
+        add(C, TOTAL_C_AT)
+        par_got[B] = scalar_gather(par_win[B], "par_got_b")
         difference(B)
+        root(C)
+        product(C)
         scatter_and_store(B)
-        scalar_gather_par(C)
-        total[D] = placed("total_d", S, TOTAL_AT[D])
-        nc.gpsimd.tensor_tensor(total[D][:], ssq_got[D][:], y_sq[D][:], ALU.add)
-        copy_y(D)
-        scalar_gather_par(D)
-        round_part(A, 1)
-        root_d = [placed("inv_root_d%d" % h, half, ROOT_D_AT + h) for h in range(2)]
-        for h, cols in enumerate(entry_halves):
-            nc.scalar.activation(root_d[h][:], total[D][:, cols], ACT.Abs_reciprocal_sqrt)
+
+        ssq_got[D] = scalar_gather(ssq_win[D], "ssq_got_d", SSQ_GOT_D_AT)
+        add(D, TOTAL_D_AT)
+        par_got[C] = scalar_gather(par_win[C], "par_got_c")
         difference(C)
+        root(D)
+        product(D)
         scatter_and_store(C)
-        step[D] = placed("step_d", S, STEP_AT[D])
-        nc.gpsimd.tensor_tensor(step[D][:, first], y_sb[D][:, first], root_d[0][:], ALU.mult)
-        round_part(B, 0, nc.gpsimd.tensor_copy)
+
         round_part(A, 0)
-        nc.gpsimd.tensor_tensor(step[D][:, second], y_sb[D][:, second], root_d[1][:], ALU.mult)
+        par_got[D] = scalar_gather(par_win[D], "par_got_d")
+        difference(D)
         scatter_and_store(D)
-        round_part(B, 1)
-        for h in range(2):
-            round_part(C, h)
+        round_part(B, 0)
+        round_part(B, 1, nc.gpsimd.tensor_copy)
+        round_part(A, 1)
+        round_part(C, 0)
+        round_part(C, 1, nc.gpsimd.tensor_copy)
 
         edges = (0, 256, 512, 768, 896, 1024)
         chunks = [slice(a, b) for a, b in zip(edges, edges[1:])]

@@ -29,15 +29,18 @@ W_BF_AT = 24
 WORD_AT = 78
 SCALE_AT = 44
 CODES_AT = 43
-SSQ_AT = (14, 18, 26, 82)
-PAR_AT = (32, 22, 78, 40)
+SSQ_AT = (32, 14, 26, 82)
+PAR_AT = (18, 22, 78, 40)
+TOTAL_AT = (52, 55)
+SQUARE_AT = {C: 52, D: 56}
+SSQ_GOT_C_AT = 54
 SQUARE_B_AT = 60
 STEP_A_AT = (60, 64)
+STEP_B_AT = 59
 TOTAL_C_AT = 64
 TOTAL_D_AT = 100
 STEP_D_AT = 104
-SSQ_GOT_D_AT = 96
-ROUNDED_AT = (94, 104)
+ROUNDED_AT = (97, 104)
 
 
 def tile_picked_adagr8_none_po_kernel(
@@ -118,7 +121,7 @@ def tile_picked_adagr8_none_po_kernel(
         for i, t in enumerate(ROW):
             w_cols = slice(t * P, (t + 1) * P)
             y_banks[i] = []
-            for cols in entry_halves if i == A else [slice(0, S)]:
+            for cols in entry_halves if i in (A, B) else [slice(0, S)]:
                 bank = psum.tile([P, cols.stop - cols.start], F32, name="y%d_%d" % (t, cols.start))
                 nc.tensor.matmul_mx(
                     out=bank[:],
@@ -153,7 +156,7 @@ def tile_picked_adagr8_none_po_kernel(
             nc.sync.dma_start(ssq_win[i][:], ssq_rows[:, ROW[i], :])
 
         for load, i in (
-            (load_par, A), (load_ssq, A), (load_ssq, B), (load_ssq, C),
+            (load_ssq, A), (load_ssq, B), (load_par, A), (load_ssq, C),
             (load_par, B), (load_ssq, D), (load_par, C), (load_par, D),
         ):
             load(i)
@@ -168,7 +171,8 @@ def tile_picked_adagr8_none_po_kernel(
 
         def product(i):
             step[i] = placed("step_d", S, STEP_D_AT) if i == D else own("step%d" % i)
-            nc.vector.tensor_tensor(step[i][:], y_banks[i][0][1][:], inv_root[i][:], ALU.mult)
+            for cols, bank in y_banks[i]:
+                nc.vector.tensor_tensor(step[i][:, cols], bank[:], inv_root[i][:, cols], ALU.mult)
 
         def add(i, at):
             total[i] = placed("total%d" % i, S, at)
@@ -192,8 +196,9 @@ def tile_picked_adagr8_none_po_kernel(
             copy(rounded[h][:, :, ROW[i]], par_win[i][:, parts[h]])
 
         half = S // 2
-        par_got[A] = own("par_got_a")
-        nc.vector.tensor_copy(par_got[A][:], par_win[A][:].indirect(ent_sb[:]))
+        ssq_got[A] = own("ssq_got_a")
+        for cols in entry_halves:
+            nc.vector.tensor_copy(ssq_got[A][:, cols], ssq_win[A][:].indirect(entries(cols)))
 
         for i in (A, B, C, D):
             inv_root[i] = own("inv_root%d" % i)
@@ -201,31 +206,33 @@ def tile_picked_adagr8_none_po_kernel(
         for cols, bank in y_banks[A]:
             nc.scalar.activation(y_sq[A][:, cols], bank[:], ACT.Square)
         y_sq_b = [placed("y_sq_b%d" % h, half, SQUARE_B_AT + h) for h in range(2)]
-        for h, cols in enumerate(entry_halves):
-            nc.scalar.activation(y_sq_b[h][:], y_banks[B][0][1][:, cols], ACT.Square)
-        total[A] = own("total_a")
+        for h, (cols, bank) in enumerate(y_banks[B]):
+            nc.scalar.activation(y_sq_b[h][:], bank[:], ACT.Square)
+        total[A] = placed("total_a", S, TOTAL_AT[A])
         for cols in entry_halves:
-            nc.vector.tensor_tensor(total[A][:, cols], ssq_win[A][:].indirect(entries(cols)), y_sq[A][:, cols], ALU.add)
-        total[B] = own("total_b")
+            nc.vector.tensor_tensor(total[A][:, cols], ssq_got[A][:, cols], y_sq[A][:, cols], ALU.add)
+        total[B] = placed("total_b", S, TOTAL_AT[B])
         for h, cols in enumerate(entry_halves):
             nc.vector.tensor_tensor(total[B][:, cols], ssq_win[B][:].indirect(entries(cols)), y_sq_b[h][:], ALU.add)
         for cols in entry_halves:
             root(A, cols)
         root(B)
         for i in (C, D):
-            y_sq[i] = own("y_sq%d" % i)
+            y_sq[i] = placed("y_sq%d" % i, S, SQUARE_AT[i])
             nc.scalar.activation(y_sq[i][:], y_banks[i][0][1][:], ACT.Square)
 
         step_a = [placed("step_a%d" % h, half, STEP_A_AT[h]) for h in range(2)]
         for h, (cols, bank) in enumerate(y_banks[A]):
             nc.vector.tensor_tensor(step_a[h][:], bank[:], inv_root[A][:, cols], ALU.mult)
         new[A] = own("new_a")
+        step[B] = placed("step_b", S, STEP_B_AT)
         for h, cols in enumerate(entry_halves):
-            nc.vector.tensor_tensor(new[A][:, cols], par_got[A][:, cols], step_a[h][:], ALU.subtract)
-        product(B)
+            nc.vector.tensor_tensor(new[A][:, cols], par_win[A][:].indirect(entries(cols)), step_a[h][:], ALU.subtract)
+        for cols, bank in y_banks[B]:
+            nc.vector.tensor_tensor(step[B][:, cols], bank[:], inv_root[B][:, cols], ALU.mult)
         scatter_and_store(A)
 
-        ssq_got[C] = scalar_gather(ssq_win[C], "ssq_got_c")
+        ssq_got[C] = scalar_gather(ssq_win[C], "ssq_got_c", SSQ_GOT_C_AT)
         add(C, TOTAL_C_AT)
         par_got[B] = scalar_gather(par_win[B], "par_got_b")
         difference(B)
@@ -233,7 +240,7 @@ def tile_picked_adagr8_none_po_kernel(
         product(C)
         scatter_and_store(B)
 
-        ssq_got[D] = scalar_gather(ssq_win[D], "ssq_got_d", SSQ_GOT_D_AT)
+        ssq_got[D] = scalar_gather(ssq_win[D], "ssq_got_d")
         add(D, TOTAL_D_AT)
         par_got[C] = scalar_gather(par_win[C], "par_got_c")
         difference(C)
@@ -241,7 +248,7 @@ def tile_picked_adagr8_none_po_kernel(
         product(D)
         scatter_and_store(C)
 
-        round_part(A, 0)
+        round_part(A, 0, nc.gpsimd.tensor_copy)
         par_got[D] = scalar_gather(par_win[D], "par_got_d")
         difference(D)
         scatter_and_store(D)

from contextlib import ExitStack

import concourse.mybir as mybir

K, T, S, N, U = 512, 2048, 512, 512, 1024
FLOPS = 2 * K * N * S

F32 = mybir.dt.float32
BF16 = mybir.dt.bfloat16
I32 = mybir.dt.int32
U32 = mybir.dt.uint32
U16 = mybir.dt.uint16
U8 = mybir.dt.uint8
FP8X4 = mybir.dt.float8_e4m3fn_x4
ALU = mybir.AluOpType
ACT = mybir.ActivationFunctionType

P = 128
PACK = 4
GROUP = 16
QUAD = 32

A, B, C, D = range(PACK)
ROW = (0, 2, 3, 1)

KB = 1024
W_RAW_AT = (48, 16)
W_BF_AT = 24
WORD_AT = 78
SCALE_AT = 44
CODES_AT = 43
SSQ_AT = (32, 14, 26, 82)
PAR_AT = (18, 22, 78, 40)
TOTAL_AT = (52, 55)
SQUARE_AT = {C: 52, D: 56}
SSQ_GOT_C_AT = 54
SQUARE_B_AT = 60
STEP_A_AT = (60, 64)
STEP_B_AT = 59
TOTAL_C_AT = 64
TOTAL_D_AT = 100
STEP_D_AT = 104
ROUNDED_AT = (97, 104)


def tile_picked_adagr8_none_po_kernel(
    tc, x_words, x_scales, w1, par, ssq, offs, ent, out_0, out_1, out_2
):
    nc = tc.nc
    with ExitStack() as ctx:
        lists = ctx.enter_context(tc.tile_pool(name="lists", bufs=1))
        held = ctx.enter_context(tc.tile_pool(name="held", bufs=1))
        arena = ctx.enter_context(tc.tile_pool(name="arena", bufs=1))
        psum = ctx.enter_context(tc.psum_pool(name="psum", bufs=1))

        offs_sb = lists.tile([P, S // GROUP], U16, name="offs_sb")
        ent_sb = lists.tile([P, S // GROUP], U16, name="ent_sb")

        w_half = N // 2
        w_rows = w1.rearrange("(p j) c -> p j c", j=PACK)
        w_raw = [arena.tile([P, PACK, w_half], F32, name="w_raw%d" % h, offset=W_RAW_AT[h] * KB) for h in range(2)]
        nc.sync.dma_start(w_raw[0][:], w_rows[:, :, :w_half])
        nc.sync.dma_start(offs_sb[:], offs)

        scale_win = arena.tile([P, T], U8, name="scale_win", align_bytes=64, offset=SCALE_AT * KB)
        nc.vector.memset(scale_win[:].bitcast(I32), 0)
        for e in range(2):
            nc.sync.dma_start(scale_win[e:P:GROUP, :].bitcast(I32), x_scales[0, e:16:2, :].bitcast(I32))

        warm = held.tile([P, 1], F32, name="warm")
        warm_out = held.tile([P, 1], F32, name="warm_out")
        nc.gpsimd.memset(warm[:], 1.0)
        nc.scalar.activation(warm_out[:], warm[:], ACT.Abs_reciprocal_sqrt)

        nc.sync.dma_start(w_raw[1][:], w_rows[:, :, w_half:])
        word_win = arena.tile([P, T], I32, name="word_win", align_bytes=64, offset=WORD_AT * KB)
        nc.sync.dma_start(word_win[:], x_words[0].rearrange("p n t -> p (n t)").bitcast(I32))
        nc.sync.dma_start(ent_sb[:], ent)

        par_rows = par.rearrange("(p t) u -> p t u", t=PACK)
        ssq_rows = ssq.rearrange("(p t) u -> p t u", t=PACK)
        out_rows = out_0.rearrange("(p t) u -> p t u", t=PACK)

        scale_got = held.tile([P, S], U8, name="scale_got", align_bytes=64)
        nc.vector.tensor_copy(scale_got[:], scale_win[:].indirect(offs_sb[:]))
        x_scale = held.tile([P, S], U8, name="x_scale", align_bytes=64)
        nc.vector.tensor_copy(x_scale[:].bitcast(I32), scale_got[:].bitcast(I32))
        for e in range(2):
            nc.scalar.dma_start(
                x_scale[2 + e : P : QUAD, :].bitcast(I32), scale_got[GROUP + e : P : QUAD, :].bitcast(I32)
            )

        w_bf = arena.tile([P, PACK, P, PACK], BF16, name="w_bf", align_bytes=64, offset=W_BF_AT * KB)
        w_quarter = N // 4
        shares = (
            (nc.scalar.copy, 0, w_raw[0][:]),
            (nc.vector.tensor_copy, w_half, w_raw[1][:, :, :w_quarter]),
            (nc.gpsimd.tensor_copy, w_half + w_quarter, w_raw[1][:, :, w_quarter:]),
        )
        for copy, start, source in shares:
            m_cols = slice(start // PACK, (start + source.shape[2]) // PACK)
            copy(
                w_bf[:, :, m_cols, :].rearrange("p t m j -> p m t j"),
                source.rearrange("p j (m t) -> p m t j", t=PACK),
            )
        w_codes = held.tile([P, N], U32, name="w_codes", align_bytes=64)
        w_scale = held.tile([P, N], U8, name="w_scale", align_bytes=64)
        nc.vector.quantize_mx(
            out=w_codes[:].bitcast(FP8X4),
            scales=w_scale[:],
            in_=w_bf[:].rearrange("p t m j -> p (t m j)"),
        )

        x_codes = arena.tile([P, S], U32, name="x_codes", align_bytes=64, offset=CODES_AT * KB)
        entry_halves = [slice(h * S // 2, (h + 1) * S // 2) for h in range(2)]
        for cols in entry_halves:
            picks = offs_sb[:, cols.start // GROUP : cols.stop // GROUP]
            nc.vector.tensor_copy(x_codes[:, cols], word_win[:].bitcast(U32).indirect(picks))

        y_banks = {}
        for i, t in enumerate(ROW):
            w_cols = slice(t * P, (t + 1) * P)
            y_banks[i] = []
            for cols in entry_halves if i in (A, B) else [slice(0, S)]:
                bank = psum.tile([P, cols.stop - cols.start], F32, name="y%d_%d" % (t, cols.start))
                nc.tensor.matmul_mx(
                    out=bank[:],
                    lhsT=w_codes[:, w_cols].bitcast(FP8X4),
                    lhsT_scale=w_scale[:, w_cols],
                    rhs=x_codes[:, cols].bitcast(FP8X4),
                    rhs_scale=x_scale[:, cols],
                    start=True,
                    stop=True,
                )
                y_banks[i].append((cols, bank))

        par_win, ssq_win, y_sq, total, inv_root = {}, {}, {}, {}, {}
        par_got, ssq_got, step, new, rounded = {}, {}, {}, {}, {}
        whole = slice(0, S)

        def entries(cols):
            return ent_sb[:, cols.start // GROUP : cols.stop // GROUP]

        def placed(name, width, at):
            return arena.tile([P, width], F32, name=name, offset=int(at * KB))

        def own(name, width=S):
            return held.tile([P, width], F32, name=name)

        def load_par(i):
            par_win[i] = placed("par_win%d" % i, U, PAR_AT[i])
            nc.sync.dma_start(par_win[i][:], par_rows[:, ROW[i], :])

        def load_ssq(i):
            ssq_win[i] = placed("ssq_win%d" % i, U, SSQ_AT[i])
            nc.sync.dma_start(ssq_win[i][:], ssq_rows[:, ROW[i], :])

        for load, i in (
            (load_ssq, A), (load_ssq, B), (load_par, A), (load_ssq, C),
            (load_par, B), (load_ssq, D), (load_par, C), (load_par, D),
        ):
            load(i)

        def scalar_gather(window, name, at=None):
            got = own(name) if at is None else placed(name, S, at)
            nc.scalar.activation(got[:], window[:].indirect(ent_sb[:]), ACT.Copy)
            return got

        def root(i, cols=whole):
            nc.scalar.activation(inv_root[i][:, cols], total[i][:, cols], ACT.Abs_reciprocal_sqrt)

        def product(i):
            step[i] = placed("step_d", S, STEP_D_AT) if i == D else own("step%d" % i)
            for cols, bank in y_banks[i]:
                nc.vector.tensor_tensor(step[i][:, cols], bank[:], inv_root[i][:, cols], ALU.mult)

        def add(i, at):
            total[i] = placed("total%d" % i, S, at)
            nc.gpsimd.tensor_tensor(total[i][:], ssq_got[i][:], y_sq[i][:], ALU.add)

        def difference(i):
            new[i] = own("new%d" % i)
            nc.gpsimd.tensor_tensor(new[i][:], par_got[i][:], step[i][:], ALU.subtract)

        def scatter_and_store(i):
            nc.vector.tensor_copy(par_win[i][:].indirect(ent_sb[:]), new[i][:])
            nc.sync.dma_start(out_rows[:, ROW[i], :], par_win[i][:])

        parts = (slice(0, U // 2), slice(U // 2, U))

        def round_part(i, h, copy=nc.scalar.copy):
            if h not in rounded:
                rounded[h] = arena.tile(
                    [P, U // 2, PACK], BF16, name="rounded%d" % h, align_bytes=64, offset=ROUNDED_AT[h] * KB
                )
            copy(rounded[h][:, :, ROW[i]], par_win[i][:, parts[h]])

        half = S // 2
        ssq_got[A] = own("ssq_got_a")
        for cols in entry_halves:
            nc.vector.tensor_copy(ssq_got[A][:, cols], ssq_win[A][:].indirect(entries(cols)))

        for i in (A, B, C, D):
            inv_root[i] = own("inv_root%d" % i)
        y_sq[A] = own("y_sq_a")
        for cols, bank in y_banks[A]:
            nc.scalar.activation(y_sq[A][:, cols], bank[:], ACT.Square)
        y_sq_b = [placed("y_sq_b%d" % h, half, SQUARE_B_AT + h) for h in range(2)]
        for h, (cols, bank) in enumerate(y_banks[B]):
            nc.scalar.activation(y_sq_b[h][:], bank[:], ACT.Square)
        total[A] = placed("total_a", S, TOTAL_AT[A])
        for cols in entry_halves:
            nc.vector.tensor_tensor(total[A][:, cols], ssq_got[A][:, cols], y_sq[A][:, cols], ALU.add)
        total[B] = placed("total_b", S, TOTAL_AT[B])
        for h, cols in enumerate(entry_halves):
            nc.vector.tensor_tensor(total[B][:, cols], ssq_win[B][:].indirect(entries(cols)), y_sq_b[h][:], ALU.add)
        for cols in entry_halves:
            root(A, cols)
        root(B)
        for i in (C, D):
            y_sq[i] = placed("y_sq%d" % i, S, SQUARE_AT[i])
            nc.scalar.activation(y_sq[i][:], y_banks[i][0][1][:], ACT.Square)

        step_a = [placed("step_a%d" % h, half, STEP_A_AT[h]) for h in range(2)]
        for h, (cols, bank) in enumerate(y_banks[A]):
            nc.vector.tensor_tensor(step_a[h][:], bank[:], inv_root[A][:, cols], ALU.mult)
        new[A] = own("new_a")
        step[B] = placed("step_b", S, STEP_B_AT)
        for h, cols in enumerate(entry_halves):
            nc.vector.tensor_tensor(new[A][:, cols], par_win[A][:].indirect(entries(cols)), step_a[h][:], ALU.subtract)
        for cols, bank in y_banks[B]:
            nc.vector.tensor_tensor(step[B][:, cols], bank[:], inv_root[B][:, cols], ALU.mult)
        scatter_and_store(A)

        ssq_got[C] = scalar_gather(ssq_win[C], "ssq_got_c", SSQ_GOT_C_AT)
        add(C, TOTAL_C_AT)
        par_got[B] = scalar_gather(par_win[B], "par_got_b")
        difference(B)
        root(C)
        product(C)
        scatter_and_store(B)

        ssq_got[D] = scalar_gather(ssq_win[D], "ssq_got_d")
        add(D, TOTAL_D_AT)
        par_got[C] = scalar_gather(par_win[C], "par_got_c")
        difference(C)
        root(D)
        product(D)
        scatter_and_store(C)

        round_part(A, 0, nc.gpsimd.tensor_copy)
        par_got[D] = scalar_gather(par_win[D], "par_got_d")
        difference(D)
        scatter_and_store(D)
        round_part(B, 0)
        round_part(B, 1, nc.gpsimd.tensor_copy)
        round_part(A, 1)
        round_part(C, 0)
        round_part(C, 1, nc.gpsimd.tensor_copy)

        edges = (0, 256, 512, 768, 896, 1024)
        chunks = [slice(a, b) for a, b in zip(edges, edges[1:])]

        def rounded_chunk(cols):
            h = max(n for n, part in enumerate(parts) if part.start <= cols.start)
            return rounded[h][:, cols.start - parts[h].start : cols.stop - parts[h].start, :]

        for cols in chunks[2:]:
            nc.scalar.copy(rounded_chunk(cols)[:, :, ROW[D]], par_win[D][:, cols])
        for cols in chunks[:2]:
            nc.vector.tensor_copy(rounded_chunk(cols)[:, :, ROW[D]], par_win[D][:, cols])

        out_codes = held.tile([P, U], U32, name="out_codes", align_bytes=64)
        out_scale = held.tile([P, U], U8, name="out_scale", align_bytes=64)
        words_hbm = out_1[0].rearrange("p n t -> p (n t)").bitcast(I32)
        stored = 0
        for c, cols in enumerate(chunks):
            nc.vector.quantize_mx(
                out=out_codes[:, cols].bitcast(FP8X4),
                scales=out_scale[:, cols],
                in_=rounded_chunk(cols).rearrange("p u t -> p (u t)"),
            )
            if c not in (0, 2):
                nc.sync.dma_start(words_hbm[:, stored : cols.stop], out_codes[:, stored : cols.stop].bitcast(I32))
                stored = cols.stop
        for q in range(P // QUAD):
            queue = nc.scalar if q % 2 == 0 else nc.sync
            queue.dma_start(
                out_2[0, 4 * q : 4 * q + 4, :].bitcast(I32), out_scale[QUAD * q : QUAD * q + 4, :].bitcast(I32)
            )
